import numpy as np, ml_dtypes
CORES = [2,6,10,14,18,22,26,30]
N = 8
import mx_ref
BF = ml_dtypes.bfloat16
def gcols(t, e):
    v = np.concatenate([t.reshape(8, 16, -1, 4), np.zeros((8, 16, 1, 4), BF)], axis=2)
    return np.ascontiguousarray(np.stack([v[g][:, e[g]] for g in range(8)])).reshape(128, -1)
def tile(rs):
    return np.stack(rs, axis=2).reshape(128, -1).astype(BF)
def pick(q, e):
    c = np.concatenate([q[0].reshape(128, -1, 4), np.zeros((128, 1, 4), np.uint8)], axis=1); s = np.concatenate([q[1], np.ones((16, 1), np.uint8)], axis=1)
    return (np.ascontiguousarray(c[:, e].reshape(128, -1)), np.ascontiguousarray(s[:, e]))
def join(*qs):
    return (np.concatenate([q[0] for q in qs], axis=1), np.concatenate([q[1] for q in qs], axis=1))
def put(q, e, v):
    c, s = q[0].reshape(128, -1, 4).copy(), q[1].copy(); c[:, e] = v[0].reshape(128, -1, 4); s[:, e] = v[1]
    return (c.reshape(128, -1), s)
def pk(c, s):
    return (np.ascontiguousarray(c), mx_ref.live(s))
def emit(q):
    return q[0], q[1]
def packed(v, rng):
    q = [mx_ref.quantize(np.ascontiguousarray(v[r])) for r in range(N)]
    return np.stack([a for a, b in q]), np.stack([mx_ref.plane(b, rng) for a, b in q])
def values_of_codes():
    e, c = np.zeros((128, 128, 4), np.float32), np.zeros((128, 2, 4), np.uint8)
    e[np.arange(128), np.arange(128), 0] = 1
    c[:127, :, 0] = np.arange(256).reshape(2, 128).T[:127]
    return mx_ref.matmul(mx_ref.quantize(e.reshape(128, 512).astype(BF)), (c.reshape(128, 8), np.full((16, 2), 127, np.uint8))).T.reshape(-1).astype(np.float64)
CODE_VALUE, SCALE_VALUE = values_of_codes(), 2.0 ** (np.arange(256) - 127.0)
def decode(q):
    return (CODE_VALUE[q[0]].reshape(16, 8, -1, 4) * SCALE_VALUE[q[1]][:, None, :, None] + 0.0).reshape(128, -1).astype(np.float32)
def f(rng, *shape):
    return mx_ref.flush((rng.standard_normal(shape, dtype=np.float32) * np.exp2(rng.integers(-2, 3, shape[:-1] + (1,)))).astype(BF))
def wide(rng, *shape, cols=0):
    v = rng.standard_normal(shape, dtype=np.float32) * np.exp2(rng.integers(-12, 13, shape)).astype(np.float32)
    if cols: v *= np.repeat(np.exp2(rng.integers(-cols, cols + 1, shape[:-2] + (1, shape[-1] // 4))) * (rng.random(shape[:-2] + (1, shape[-1] // 4)) > 0.0625), 4, axis=-1).astype(np.float32)
    return mx_ref.flush(v.astype(BF))
C, R = 384, 2
STEP = [1, 2]
def maxima(p):
    h = p[::16]
    m = np.zeros((8, C), bool)
    m[:, 1:-1] = (h[:, 1:-1] > h[:, :-2]) & (h[:, 1:-1] >= h[:, 2:])
    return m
def brackets(m):
    j = np.arange(C)
    a = np.maximum.accumulate(np.where(m, j, -1), axis=1)
    b = np.full((8, C), C - 1)
    b[:, :-1] = np.minimum.accumulate(np.where(m, j, C - 1)[:, ::-1], axis=1)[:, ::-1][:, 1:]
    return a, b, np.where(a[:, -1:] < 0, C - 1, a[:, -1:])
def half(s, t):
    return ((s.astype(np.float32) + t.astype(np.float32)) * np.float32(0.5)).astype(BF)
def numbers_of(rng):
    return {"x": np.array(f(rng, N, 128, 4 * C)), "u": np.array(f(rng, N, 128, 512)), "v": np.array(f(rng, N, 128, 512))}
def weights(rng, still=[]):
    w = np.array(f(rng, N, 128, 2048)).reshape(N, 8, 16, 4, 8, 16, 4)
    for i in still:
        w[:, :, i] = 0
        w[:, :, :, :, :, i] = 0
    c, p = packed(w.reshape(N, 128, 2048), rng)
    return {"wc": c, "ws": p}
def signs(rng):
    return np.stack([rng.permutation(8) % 2 * 2.0 - 1.0 for r in range(N)])
def setup_inputs(rng):
    return {**numbers_of(rng), **weights(rng)}
def setup_inputs_ties(rng):
    d = numbers_of(rng)
    e = rng.permutation(N)
    x = d["x"].reshape(N, 8, 16, C, 4)
    for r in range(N):
        k = np.zeros(C, int) if r == e[0] else rng.permutation(C) % 3
        a = x[r][:, :8, :3].copy()
        a[:, :, 2] = 0
        x[r][:, :8] = a[:, :, k]
    x[e[1]] = 0
    u = d["u"].reshape(N, 8, 16, 8, 16, 4)
    k = u.copy()
    u[:, :, :, :, 0] = 0
    for g in range(8): u[:, g, :8, g, 0] = k[:, g, :8, g, 0]
    return {"x": x.reshape(N, 128, 4 * C), "u": u.reshape(N, 128, 512), "v": d["v"], **weights(rng, range(8))}
def setup_inputs_near(rng):
    d = numbers_of(rng)
    x = d["x"].astype(np.float32).reshape(N, 8, 16, C, 4)
    u = d["u"].reshape(N, 128, 128, 4)
    u[:, :, ::16] = 0
    x[:, :, 0] = 0
    x[:, :, 8] = 0
    o, c = rng.permutation(N) % 4, signs(rng)
    for r in range(N):
        q = 2.0 ** -23 if o[r] < 2 else 2.0 ** -26
        if o[r] < 2: x[r, :, 0, :, 0] = c[r][:, None]
        s = rng.integers(0, 4, (8, C))
        s[:, :13] = [0, 2, 3, 3, 2, 2, 0, 1, 0, 1, 2, 0, 3]
        x[r, :, 8, :, 0] = s * q
        x[r, :, 9:] = rng.integers(4, 8, (8, 7, C, 4)) * q
        if o[r] == 3: x[r, :, 9, :, 0] = s * q
        k = 1.0 if o[r] % 2 == 0 else 2.0 ** -30
        for h in range(0, 128, 16):
            u[r, h, h, 0] = k
            u[r, h + 8, h, 0] = k
            if o[r] == 3:
                u[r, h + 8, h, 0] = 1.125 * k
                u[r, h + 9, h, 0] = -k
    return {"x": x.reshape(N, 128, 4 * C).astype(BF), "u": u.reshape(N, 128, 512), "v": d["v"], **weights(rng, [0, 8, 9, 10, 11, 12, 13, 14, 15])}
def setup_inputs_shapes(rng):
    d = numbers_of(rng)
    x = d["x"].astype(np.float32).reshape(N, 8, 16, C, 4)
    u = d["u"].reshape(N, 128, 128, 4)
    x[:, :, :11] = 0
    x[:, :, :8] = (9 + 4 * rng.integers(0, 2, (N, 8, 8, C, 4))) * np.exp2(-8.0 - np.arange(32).reshape(8, 1, 4) % 13)
    x[:, :, 0, :, 0] = 1.96875
    u[:, :, ::16] = 0
    j = np.arange(C)
    n = np.stack([rng.permutation(8) for r in range(N)])
    n[1] = n[0]
    size = np.where(rng.permutation(N) < N // 2, 2.0 ** -30, 1.0) * np.where(rng.permutation(N) < N // 2, -1.0, 1.0)
    for r in range(N):
        m = (1, C - 2)[r % 2]
        key = np.stack([0 * j + 5, j, C - 1 - np.abs(j - m), np.abs(j - m), j % 2, j // 2, (C - 1 - j) // 3, ((j == 1) | (j == C - 2)) + 0])[n[r]]
        z = ((key[:, :, None] >> np.arange(12)) & 1) * np.exp2(np.arange(12.0))
        for i in range(3): x[r, :, 8 + i] = z[:, :, 4 * i:4 * i + 4]
        for h in range(0, 128, 16): u[r, h + 8:h + 11, h] = size[r]
    return {"x": x.reshape(N, 128, 4 * C).astype(BF), "u": u.reshape(N, 128, 512), "v": d["v"], **weights(rng, range(11))}
def setup_inputs_huge(rng):
    d = numbers_of(rng)
    x = 0.55 + 0.35 * rng.random((N, 128, C, 4))
    a = 2.0 ** 30 * (1 - 0.1 * rng.random((N, 128, 8, 4))) * signs(rng)[:, None, :, None]
    h = np.where(np.arange(128) < 64, 1.0, -1.0)
    for r in rng.permutation(N)[:N // 2]:
        c = rng.permutation(C) % 2 * 2.0 - 1.0
        x[r] = 0.7 + 0.05 * rng.random((128, C, 4)) + 0.15 * h[:, None, None] * c[:, None]
        a[r] *= h[:, None, None]
    u = d["u"].reshape(N, 128, 128, 4)
    u[:, :, ::16] = a.astype(np.float32).astype(BF)
    w = np.zeros((N, 128, 4, 128, 4), np.float32)
    i = np.arange(128)
    for b in range(4): w[:, i, b, i, b] = 0.125
    wc, ws = packed(w.reshape(N, 128, 2048).astype(BF), rng)
    return {"x": (x * 2.0 ** 30).astype(np.float32).reshape(N, 128, 4 * C).astype(BF), "u": u.reshape(N, 128, 512), "v": d["v"], "wc": wc, "ws": ws}
def setup_inputs_spread(rng):
    d = setup_inputs(rng)
    d["x"] = wide(rng, N, 128, 4 * C, cols=6)
    return d
def check_inputs(d):
    b = []
    for k in ("x", "u", "v"):
        a = np.abs(d[k].astype(np.float32))
        if not (np.isfinite(a).all() and ((a == 0) | (a >= 2.0 ** -30) & (a <= 2.0 ** 30)).all()): b.append("a value of " + k)
    if ((d["wc"] & 0x7F) == 0x7F).any(): b.append("a code of wc that is no number")
    z = np.zeros((128, 4, 4), np.float32)
    z[:, 1] = 2.0 ** -30
    z[:, 2] = 2.0 ** 30
    c, s = emit(mx_ref.quantize(z.reshape(128, 16).astype(BF)))
    for r in range(N):
        p = mx_ref.live(d["ws"][r])
        if not ((p == s[0, 0]) | (p >= s[0, 1]) & (p <= s[0, 2])).all(): b.append("a scale of ws")
    return b
def reference(x, u, v, wc, ws):
    qu = [mx_ref.quantize(u[r]) for r in range(N)]
    lay = [pk(wc[r], ws[r]) for r in range(N)]
    now = [x[r] for r in range(N)]
    om = np.zeros((N, 8, C), np.float32)
    for t in range(R):
        full, ends, four, rest, sent = [], [], [], [], []
        for r in range(N):
            q = mx_ref.quantize(now[r])
            p = mx_ref.matmul(qu[r], q)
            hi, lo = maxima(p), maxima(-p)
            a, b, i = brackets(hi)
            c, d, k = brackets(lo)
            full.append(decode(q).astype(BF))
            ends.append(gcols(full[r], np.concatenate([i, k], axis=1)))
            four.append((np.where(a < 0, C, a), b, np.where(c < 0, C + 1, c), d))
            om[r] = 1.0 + hi - lo
        for r in range(N):
            z = np.concatenate([full[r], ends[(r - 1) % N]], axis=1)
            a, b, c, d = [gcols(z, k) for k in four[r]]
            e = half(half(a, b), half(c, d))
            rest.append((full[r].astype(np.float32) - e.astype(np.float32)).astype(BF))
            sent.append(mx_ref.quantize(e))
        now = [tile([mx_ref.matmul(pick(lay[r], np.arange(128 * b, 128 * b + 128)), sent[r ^ STEP[t]]) * np.float32(0.03125) + rest[r][:, b::4].astype(np.float32) for b in range(4)]) for r in range(N)]
    y = np.zeros((N, 128, C), np.float32)
    oc, osc = np.zeros((N, 128, 4 * C), np.uint8), np.zeros((N, 16, C), np.uint8)
    for r in range(N):
        q = mx_ref.quantize(now[r])
        y[r] = mx_ref.matmul(mx_ref.quantize(v[r]), q)
        oc[r], osc[r] = emit(q)
    return {"y": y, "om": om, "oc": oc, "osc": osc}

@@ -1,0 +1,433 @@
+from concourse.bass import DstId, RemoteDMATransfer
+from concourse.mybir import dt, AluOpType, ActivationFunctionType
+
+C = 384
+ROUNDS = 2
+STEP = [1, 2]
+CUT = [192, 192, 192]
+EARLY = [1]
+XO = 16
+
+X4, U8, BF, F32, I32, U16 = "float8_e4m3fn_x4", "uint8", "bfloat16", "float32", "int32", "uint16"
+
+
+def _scratch():
+    s = {}
+
+    def sb(name, n, d):
+        s[name] = ("sbuf", [128, n], d)
+
+    for t in range(ROUNDS + 1):
+        sb("xb%d" % t, XO + 4 * C, BF)
+        sb("qx%d" % t, C + 16, X4)
+        sb("sx%d" % t, C + 16, U8)
+    for t in range(ROUNDS):
+        sb("qn%d" % t, 128, X4)
+        sb("sn%d" % t, 128, U8)
+        sb("qe%d" % t, C, X4)
+        sb("se%d" % t, C, U8)
+        sb("ql%d" % t, C, X4)
+        sb("sl%d" % t, C, U8)
+        sb("e%d" % t, 4 * C, BF)
+    for name, n, d in [
+        ("ub", 512, BF), ("qu", 128, X4), ("su", 128, U8), ("qup", 128, X4), ("sup", 128, U8),
+        ("vb", 512, BF), ("qv", 128, X4), ("sv", 128, U8), ("qw", 512, X4), ("sw", 512, U8),
+        ("idm", 128, F32), ("z", 1040, BF), ("qz", 1024, X4), ("sz", 1024, U8),
+        ("uli", 8, I32), ("ul", 8, U16), ("ci", 128, F32), ("ct", 128, F32), ("cs", 24, F32),
+        ("tfi", 400, BF), ("tf", 400, BF), ("tki", 400, BF), ("tk", C, BF), ("mi", 192, BF), ("mm", C, BF),
+        ("lci", 4, F32), ("lc", 4, U16),
+        ("pc", C, F32), ("pb", C, F32), ("df", C, BF), ("gg", C, BF), ("hi", C, BF), ("fb", 2 * C, BF), ("sel", C, BF),
+        ("kb", C + 32, BF), ("tr", 2 * C + 32, BF), ("la", 24, U16), ("lb", 24, U16), ("i2", 64, U16), ("eo", 2, U16),
+        ("fq", 4 * C, BF), ("tt", 4 * C, BF), ("sab", 4 * C, BF), ("uu", 4 * C, BF), ("e32", 4 * C, BF),
+        ("g32", 4 * C, BF), ("x32", 4 * C, BF), ("omv", C, F32), ("yb", C, F32),
+    ]:
+        sb(name, n, d)
+    s["ps"] = ("psum", [128, 4096], F32)
+    return s
+
+
+SCRATCH = _scratch()
+POOLS = {"c": 100, "h": 20, "s": 2}
+SEMAPHORES = ([k + str(i) for k in POOLS for i in range(POOLS[k])] + ["sent"]
+              + ["ends%d" % t for t in range(ROUNDS)]
+              + ["mean%d_%d" % (t, j) for t in range(ROUNDS) for j in range(2)])
+
+
+def _mask(engines):
+    return sum(1 << e for e in engines)
+
+
+def emit(ops, queues, T):
+    groups = {}
+    for i, o in enumerate(ops):
+        groups.setdefault(o["grp"], []).append(i)
+    known = {q: set() for q in queues}
+    for i, o in enumerate(ops):
+        deps = set()
+        for j in range(i):
+            p = ops[j]
+            hit = False
+            for name, m in o["w"].items():
+                hit = hit or bool(m & (p["w"].get(name, 0) | p["r"].get(name, 0)))
+            for name, m in o["r"].items():
+                hit = hit or bool(m & p["w"].get(name, 0))
+                if name == "ps" and p["q"] != o["q"]:
+                    hit = hit or bool(m & p["r"].get(name, 0))
+            if hit or p["grp"] in o["after"]:
+                deps.add(j)
+        k = known[o["q"]]
+        waits = []
+        for j in sorted(deps, reverse=True):
+            if j in k:
+                continue
+            members = groups[ops[j]["grp"]]
+            assert max(members) < i, (o["grp"], ops[j]["grp"])
+            waits.append(ops[j]["grp"])
+            for m in members:
+                k.add(m)
+                k |= ops[m]["known"]
+        o["waits"] = waits
+        o["known"] = set(k)
+    needed = set(w for o in ops for w in o["waits"])
+    last, count, where = {}, {}, {}
+    for key, members in groups.items():
+        if key not in needed:
+            continue
+        pool = ops[members[0]]["pool"]
+        for n in range(POOLS[pool]):
+            name = pool + str(n)
+            if all(a in ops[m]["known"] for m in members for a in last.get(name, [])):
+                break
+        else:
+            raise ValueError("out of semaphores")
+        last[name] = members
+        count[name] = count.get(name, 0) + sum(ops[m]["inc"] for m in members)
+        where[key] = (name, count[name])
+    for o in ops:
+        q = queues[o["q"]]
+        for name, val in [where[w] for w in o["waits"]] + o["ext"]:
+            q.wait_ge(T.sem[name], val)
+        if o["fn"] is not None:
+            ins = o["fn"]()
+            if o["grp"] in where:
+                ins.then_inc(T.sem[where[o["grp"]][0]], o["inc"])
+
+
+def rank_program(g, core, T, topo):
+    rank = T.rank_of(core)
+    if rank is None:
+        return
+    n_ranks = len(T.cores)
+    vec, act, pe = g.vector, g.scalar, g.tensor
+    queues = {"g": g, "v": vec, "a": act, "p": pe, "y": g.sync}
+    Op, Fn = AluOpType, ActivationFunctionType
+    ops = []
+
+    def A(name, a=None, b=None, s=None):
+        cols = range(*slice(a, b, s).indices(SCRATCH[name][1][1]))
+        m = 0
+        for c in cols:
+            m |= 1 << (c // 512 if name == "ps" else c)
+        ap = T[name][:, a:b] if s is None else T[name][:, a:b:s]
+        return (ap, [(name, m)])
+
+    def ind(win, off, word=False):
+        ap = win[0].bitcast(dt.uint32) if word else win[0]
+        return (ap.indirect(off[0]), win[1] + off[1])
+
+    def rec(q, fn, r, w, grp=None, pool="c", inc=1, ext=(), after=()):
+        rd, wr = {}, {}
+        for d, views in ((rd, r), (wr, w)):
+            for v in views:
+                if isinstance(v, tuple):
+                    for name, m in v[1]:
+                        d[name] = d.get(name, 0) | m
+        ops.append({"q": q, "fn": fn, "r": rd, "w": wr, "grp": grp if grp else "op%d" % len(ops), "pool": pool,
+                    "inc": inc, "ext": list(ext), "after": list(after)})
+
+    def val(s):
+        return s[0] if isinstance(s, tuple) else s
+
+    def copy(o, i, **k):
+        rec("v", lambda: vec.tensor_copy(o[0], i[0]), [i], [o], **k)
+
+    def tt(o, a, b, op, **k):
+        rec("v", lambda: vec.tensor_tensor(o[0], a[0], b[0], op), [a, b], [o], **k)
+
+    def ts(o, a, s1, s2, op0, op1=None, **k):
+        if op1 is None:
+            rec("v", lambda: vec.tensor_scalar(o[0], a[0], val(s1), None, op0), [a, s1], [o], **k)
+        else:
+            rec("v", lambda: vec.tensor_scalar(o[0], a[0], val(s1), val(s2), op0, op1), [a, s1, s2], [o], **k)
+
+    def scan(o, d0, d1, first=1.0, **k):
+        rec("v", lambda: vec.tensor_tensor_scan(o[0], d0[0], d1[0], val(first), Op.add, Op.min), [d0, d1, first], [o], **k)
+
+    def transp(o, i, **k):
+        rec("v", lambda: vec.transpose(o[0], i[0]), [i], [o], **k)
+
+    def fill(o, c, **k):
+        rec("v", lambda: vec.memset(o[0], c), [], [o], **k)
+
+    def quant(qn, sn, a, b, i, **k):
+        qo, so = A(qn, a, b), A(sn, a, b)
+        rec("v", lambda: vec.quantize_mx(qo[0], so[0], i[0]), [i], [qo, so], **k)
+
+    def scal(o, i, scale=None, bias=None, **k):
+        if scale is None:
+            rec("a", lambda: act.activation(o[0], i[0], Fn.Copy), [i], [o], **k)
+        elif bias is None:
+            rec("a", lambda: act.activation(o[0], i[0], Fn.Identity, scale=val(scale)), [i, scale], [o], **k)
+        else:
+            rec("a", lambda: act.activation(o[0], i[0], Fn.Identity, bias=val(bias), scale=val(scale)),
+                [i, scale, bias], [o], **k)
+
+    def iota(o, pattern, base, cm=0, small=True, **k):
+        if small:
+            rec("g", lambda: g.iota(o[0], pattern, base, cm, allow_small_or_imprecise_dtypes=True), [], [o], **k)
+        else:
+            rec("g", lambda: g.iota(o[0], pattern, base, cm), [], [o], **k)
+
+    def mm(bank, wq, ws, w0, xq, xs, a, b, **k):
+        o = A("ps", 512 * bank, 512 * bank + b - a)
+        l, ls, r, rs = A(wq, w0, w0 + 128), A(ws, w0, w0 + 128), A(xq, a, b), A(xs, a, b)
+        rec("p", lambda: pe.matmul_mx(o[0], l[0], ls[0], r[0], rs[0], True, True), [l, ls, r, rs], [o], **k)
+
+    def dma(q, o, i, **k):
+        rec(q, lambda: queues[q].dma_start(val(o), val(i)), [i], [o], pool="h", inc=16, **k)
+
+    def bits(v):
+        return (v[0].bitcast(dt.uint8), v[1])
+
+    def P(bank, a, b, s=None):
+        return A("ps", 512 * bank + a, 512 * bank + b, s)
+
+    def win(name, b, a=0, e=C):
+        return A(name, C * b + a, C * b + e)
+
+    sent = [0]
+    H = CUT[0]
+
+    dma("a", A("ub"), T.u[:])
+    for a, b in ((0, H), (H, C)):
+        dma("y", A("xb0", XO + 4 * a, XO + 4 * b), T.x[:, 4 * a:4 * b])
+    dma("y", bits(A("qw", 0, 512)), T.wc[:], grp="w")
+    dma("y", A("sw", 0, 512), T.ws[:], grp="w")
+    dma("y", A("vb"), T.v[:])
+
+    iota(A("uli"), [[16, 8]], 0, small=False)
+    iota(A("idm"), [[1, 128]], 0, -1)
+    iota(A("ci", 0, 32), [[0, 4], [1, 8]], 0, grp="ci")
+    iota(A("ci", 32, 64), [[0, 2], [8, 2], [0, 8]], 0, grp="ci")
+    iota(A("ci", 64, 96), [[0, 8], [1, 4]], 4 * 192, grp="ci")
+    iota(A("ci", 96, 112), [[32, 8], [C + 32, 2]], 0, grp="ci")
+    iota(A("ci", 112, 128), [[32, 8], [-C, 2]], C + 16, grp="ci")
+    iota(A("tfi", 0, 400), [[1, 400]], -192)
+    iota(A("mi"), [[0, 24], [1, 8]], 0)
+    iota(A("lci"), [[8, 2], [256, 2]], 0)
+    iota(A("tki", 0, 400), [[16, 25], [1, 8], [0, 2]], -192)
+
+    fill(A("z"), 0.0)
+    fill(A("hi", 0, C, C - 1), 0.0, grp="fills")
+    fill(A("kb", 0, 16), 0.0, grp="fills")
+    fill(A("kb", C + 16, C + 32), 0.0, grp="fills")
+    fill(A("fq", 0, 4 * C, C), 0.0, grp="fills")
+    copy(A("ul"), A("uli"))
+    ts(A("z", 3, 515, 4), A("idm"), 0.0, 32.0, Op.is_equal, Op.mult)
+    ts(A("z", 523, 1035, 4), A("idm"), 0.0, 0.25, Op.is_equal, Op.mult)
+    for b in range(4):
+        quant("qz", "sz", 128 * b, 128 * b + 128, A("z", 3 - b, 515 - b), grp="z32")
+    transp(A("ct"), A("ci"))
+    c_q, c_role, c_end, c_f = A("ct", 0, 1), A("ct", 32, 33), A("ct", 64, 65), A("ct", 96, 97)
+    c_sign, c_rb, c_om = A("cs", 0, 1), A("cs", 8, 9), A("cs", 16, 17)
+    scal(c_sign, c_role, -0.25, 1.0)
+    scal(c_rb, c_role, 1.0 / 512)
+    scal(c_om, c_role, -0.125, 1.0)
+    quant("qu", "su", 0, 128, A("ub"))
+    copy((T.qup[:, 0:128].bitcast(dt.uint32), A("qup")[1]), ind(A("qu", 0, 128), A("ul", 0, 8), word=True))
+    scal(A("sup", 0, 128), ind(A("su", 0, 128), A("ul", 0, 8)))
+    scal(A("tf"), A("tfi"), 1.0 / 512)
+
+    def score_first(t):
+        mm(4, "qup", "sup", 0, "qx%d" % t, "sx%d" % t, 0, CUT[t])
+        scal(A("pc", 0, CUT[t]), P(4, 0, CUT[t]))
+
+    quant("qx0", "sx0", 0, H, A("xb0", XO, XO + 4 * H))
+    score_first(0)
+    ts(A("mm", 0, 192), A("mi"), c_q, None, Op.is_equal, grp="mm")
+    ts(A("mm", C - 1, 191, -1), A("mi"), c_q, None, Op.is_equal, grp="mm")
+    quant("qx0", "sx0", H, C, A("xb0", XO + 4 * H, XO + 4 * C))
+
+    for t in range(ROUNDS):
+        xb, qx, sx = "xb%d" % t, "qx%d" % t, "sx%d" % t
+        qn, sn, qe, se, ql, sl, e = ["%s%d" % (k, t) for k in ("qn", "sn", "qe", "se", "ql", "sl", "e")]
+        nxb, nqx, nsx = "xb%d" % (t + 1), "qx%d" % (t + 1), "sx%d" % (t + 1)
+        last = t == ROUNDS - 1
+        early = t in EARLY
+        tag = "r%d" % t
+        H = CUT[t]
+        runs = [(0, CUT[t + 1]), (CUT[t + 1], C)]
+
+        mm(5, "qup", "sup", 0, qx, sx, H - 2, C)
+        for b in range(4):
+            mm(b, "qz", "sz", 128 * b, qx, sx, 0, C)
+        scal(A("pb", H - 2, C), P(5, 0, C - H + 2), c_sign)
+        scal(A(xb, XO, XO + 4), A(xb, XO + 4 * C - 4, XO + 4 * C))
+        if t == 0:
+            scal(A("tk"), A("tki", 1, C + 1), 1.0 / 512, c_rb)
+        for b in range(4):
+            scal(win("fq", b, 1), P(b, 1, C), 1.0 / 128)
+
+        def backward():
+            scan(A("fb", C, 2 * C), A("hi", None, None, -1), A("tf", 1, C + 1))
+
+        def choose():
+            scan(A("sel"), A("mm"), A("fb", 0, 2 * C, 2))
+
+        def slot_lists():
+            ts(A("la"), A("sel", 7, 192, 8), 512.0, 192.0, Op.mult, Op.add)
+            ts(A("lb"), A("sel", C - 1, 191, -8), -512.0, 192.0, Op.mult, Op.add)
+
+        tt(A("df", 1, H), P(4, 1, H), A("pc", 0, H - 1), Op.subtract)
+        ts(A("gg", 1, H), A("df", 1, H), c_sign, 0.0, Op.mult, Op.is_gt)
+        tt(A("hi", 1, H - 1), A("gg", 1, H - 1), A("gg", 2, H), Op.is_gt)
+        tt(A("gg", H, C), A("pb", H, C), A("pb", H - 1, C - 1), Op.is_gt)
+        scan(A("fb", 0, H - 1), A("hi", 0, H - 1), A("tf", 0, H - 1))
+        tt(A("hi", H - 1, C - 1), A("gg", H - 1, C - 1), A("gg", H, C), Op.is_gt)
+        scan(A("fb", H - 1, C), A("hi", H - 1, C), A("tf", H - 1, C), A("fb", H - 2, H - 1))
+        if early:
+            backward()
+        ts(A("eo", 0, 1), A("fb", C - 1, C), 2048.0, c_end, Op.mult, Op.add)
+        if early:
+            choose()
+        copy(A(xb, 0, XO), ind(A(xb, XO, XO + 4 * C), A("eo", 0, 1)))
+        if early:
+            slot_lists()
+        quant(qn, sn, 0, 128, A(xb, 0, 512))
+
+        right = T.cores[(rank + 1) % n_ranks]
+        left = T.cores[(rank - 1) % n_ranks]
+        eng = topo.engines(core, right)
+        rid, pid = topo.addr(right)[:2]
+        half = len(eng) // 2
+
+        def send_ends(qn=qn, sn=sn, qx=qx, sx=sx, t=t, eng=eng, half=half, rid=rid, pid=pid):
+            d = DstId(rid=rid, pnc=pid)
+            return g.remote_dma_fused([
+                RemoteDMATransfer(dst_ids=[d], dma_engine_mask=_mask(eng[:half]), remote_sem=T.sem["ends%d" % t],
+                                  src=T[qn][:, 0:4].bitcast(dt.uint8), dst=T[qx][:, C:C + 4].bitcast(dt.uint8)),
+                RemoteDMATransfer(dst_ids=[d], dma_engine_mask=_mask(eng[half:]), remote_sem=T.sem["ends%d" % t],
+                                  src=T[sn][:, 0:16], dst=T[sx][:, C:C + 16]),
+            ], local_sem=T.sem.sent)
+
+        rec("g", send_ends, [A(qn, 0, 4), A(sn, 0, 16)], [])
+        sent[0] += len(eng)
+
+        if not early:
+            backward()
+            choose()
+        scan(A("kb", 16, C + 16), A("hi"), A("tk"))
+        if not early:
+            slot_lists()
+        transp(A("tr", 0, C), A("kb", 16, C + 16), grp=tag + "tr")
+        transp(A("tr", C, 2 * C + 32), A("kb"), grp=tag + "tr")
+        if t == 0:
+            ts(A("lc"), A("lci"), c_f, float(2 * C + 31), Op.add, Op.min)
+            for b in range(4):
+                quant("qz", "sz", 512 + 128 * b, 640 + 128 * b, A("z", 523 - b, 1035 - b), grp="z4")
+        ts(A("i2"), ind(A("tr"), A("lc")), 512.0, 192.0, Op.mult, Op.add)
+
+        for b in range(4):
+            mm(4 + b, "qz", "sz", 512 + 128 * b, qx, sx, C + 4 - 128, C + 4,
+               ext=[("ends%d" % t, len(topo.engines(left, core)))] if b == 0 else [])
+
+        def slots(b, a, e2):
+            tt(win("sab", b, a, e2), ind(win("fq", b), A("lb", a // 16, e2 // 16)), win("tt", b, a, e2), Op.add)
+
+        def fix(b):
+            v = A("sab", C * b, C * b + 9, 8)
+            tt(v, P(4 + b, 124, 127, 2), v, Op.add)
+
+        for b in range(4):
+            scal(win("tt", b), ind(win("fq", b), A("la")))
+        for b in range(3):
+            slots(b, 0, C)
+        slots(3, 0, 192)
+        if t == 0:
+            quant("qv", "sv", 0, 128, A("vb"))
+        fix(0)
+        slots(3, 192, C)
+        for b in range(1, 4):
+            fix(b)
+
+        mate = T.cores[rank ^ STEP[t]]
+        eng = topo.engines(core, mate)
+        rid, pid = topo.addr(mate)[:2]
+        for j, (a, b2) in enumerate(runs):
+            for b in range(4):
+                scal(win("uu", b, a, b2), ind(win("sab", b), A("i2", a // 16, b2 // 16)))
+            for b in range(4):
+                tt(A(e, 4 * a + b, 4 * b2, 4), ind(win("sab", b), A("i2", 32 + a // 16, 32 + b2 // 16)),
+                   win("uu", b, a, b2), Op.add, grp=tag + "e%d" % j)
+            quant(qe, se, a, b2, A(e, 4 * a, 4 * b2))
+            for src, dst in ((A(se, a, b2), A(sl, a, b2)), (bits(A(qe, a, b2)), bits(A(ql, a, b2)))):
+                rec("g", lambda src=src, dst=dst, j=j, t=t, eng=eng, rid=rid, pid=pid: g.remote_dma(
+                    dst[0], src[0], T.sem["mean%d_%d" % (t, j)], T.sem.sent, pid, rid, _mask(eng)), [src], [])
+                sent[0] += len(eng)
+
+        for a, b2 in runs:
+            scal(A("e32", 4 * a, 4 * b2), A(e, 4 * a, 4 * b2), 32.0)
+        for j, (a, b2) in enumerate(runs):
+            for b in range(4):
+                tt(win("g32", b, a, b2), P(b, a, b2), A("e32", 4 * a + b, 4 * b2, 4), Op.subtract,
+                   grp=tag + "g%d" % j)
+        if last:
+            scal(A("omv"), A("hi"), c_sign, c_om)
+            dma("y", T.om[:], (T.omv[0:128:16, :], A("omv")[1]), grp="om0")
+            rec("g", lambda: g.dma_start(T.om[:], T.omv[8:128:16, :], accum_op=Op.add), [A("omv")], [], grp="om1",
+                pool="s", inc=16, after=["om0"])
+
+        def product(j):
+            a, b2 = runs[j]
+            need = [("mean%d_%d" % (t, j), 2 * len(topo.engines(mate, core)))]
+            for b in range(4):
+                mm(4 * (1 - j) + b, "qw", "sw", 128 * b, ql, sl, a, b2, ext=need if b == 0 else [])
+
+        def state(j, b):
+            a, b2 = runs[j]
+            tt(win("x32", b, a, b2), P(4 * (1 - j) + b, 0, b2 - a), win("g32", b, a, b2), Op.add)
+            o, i = A(nxb, XO + 4 * a + b, XO + 4 * b2, 4), win("x32", b, a, b2)
+            if b == 3:
+                ts(o, i, 1.0 / 32, None, Op.mult)
+                quant(nqx, nsx, a, b2, A(nxb, XO + 4 * a, XO + 4 * b2))
+            else:
+                scal(o, i, 1.0 / 32)
+
+        H = CUT[t + 1]
+        product(0)
+        for b in range(4):
+            state(0, b)
+        if last:
+            mm(4, "qv", "sv", 0, nqx, nsx, 0, H)
+            dma("y", T.oc[:, 0:4 * H], bits(A(nqx, 0, H)), grp="outy")
+            scal(A("yb", 0, H), P(4, 0, H))
+            dma("y", T.y[:, 0:H], A("yb", 0, H), grp="outy")
+        product(1)
+        for b in range(3):
+            state(1, b)
+        if not last:
+            score_first(t + 1)
+        state(1, 3)
+        if last:
+            mm(5, "qv", "sv", 0, nqx, nsx, H, C)
+            dma("y", T.oc[:, 4 * H:4 * C], bits(A(nqx, H, C)), grp="outy")
+            for k in range(4):
+                dma("y" if k < 2 else "a", T.osc[4 * k:4 * k + 4, 0:C],
+                    (T[nsx][32 * k:32 * k + 4, 0:C], A(nsx, 0, C)[1]), grp="outy" if k < 2 else "outa")
+            copy(A("yb", H, C), P(5, 0, C - H))
+            dma("a", T.y[:, H:C], A("yb", H, C), grp="outa")
+
+    rec("y", None, [], [], after=["outy"])
+    rec("a", None, [], [], after=["outa"])
+    rec("g", None, [], [], after=["om1"], ext=[("sent", sent[0])])
+    emit(ops, queues, T)

@@ -4,9 +4,10 @@ from concourse.mybir import dt, AluOpType, ActivationFunctionType
 C = 384
 ROUNDS = 2
 STEP = [1, 2]
-CUT = [192, 192, 192]
-EARLY = [1]
-XO = 16
+CUT = [[192], [224], [192]]
+SPLIT = [0]
+PART = 96
+XO = 64
 
 X4, U8, BF, F32, I32, U16 = "float8_e4m3fn_x4", "uint8", "bfloat16", "float32", "int32", "uint16"
 
@@ -20,7 +21,7 @@ def _scratch():
     for t in range(ROUNDS + 1):
         sb("xb%d" % t, XO + 4 * C, BF)
         sb("qx%d" % t, C + 16, X4)
-        sb("sx%d" % t, C + 16, U8)
+        sb("sx%d" % t, C + 64, U8)
     for t in range(ROUNDS):
         sb("qn%d" % t, 128, X4)
         sb("sn%d" % t, 128, U8)
@@ -32,12 +33,12 @@ def _scratch():
     for name, n, d in [
         ("ub", 512, BF), ("qu", 128, X4), ("su", 128, U8), ("qup", 128, X4), ("sup", 128, U8),
         ("vb", 512, BF), ("qv", 128, X4), ("sv", 128, U8), ("qw", 512, X4), ("sw", 512, U8),
-        ("idm", 128, F32), ("z", 1040, BF), ("qz", 1024, X4), ("sz", 1024, U8),
-        ("uli", 8, I32), ("ul", 8, U16), ("ci", 128, F32), ("ct", 128, F32), ("cs", 24, F32),
+        ("idm", 128, F32), ("z", 1040, BF), ("qz", 640, X4), ("sz", 640, U8),
+        ("uli", 8, I32), ("ul", 8, U16), ("ci", 160, F32), ("ct", 160, F32), ("cs", 24, F32), ("ce", 4, F32),
         ("tfi", 400, BF), ("tf", 400, BF), ("tki", 400, BF), ("tk", C, BF), ("mi", 192, BF), ("mm", C, BF),
         ("lci", 4, F32), ("lc", 4, U16),
-        ("pc", C, F32), ("pb", C, F32), ("df", C, BF), ("gg", C, BF), ("hi", C, BF), ("fb", 2 * C, BF), ("sel", C, BF),
-        ("kb", C + 32, BF), ("tr", 2 * C + 32, BF), ("la", 24, U16), ("lb", 24, U16), ("i2", 64, U16), ("eo", 2, U16),
+        ("pc", C, F32), ("df", C, BF), ("gg", C, BF), ("pb", C, F32), ("hi", C, BF), ("fb", 2 * C, BF), ("sel", C, BF),
+        ("kb", C + 32, BF), ("tr", 2 * C + 32, BF), ("la", 24, U16), ("lb", 24, U16), ("i2", 64, U16), ("eo", 4, U16),
         ("fq", 4 * C, BF), ("tt", 4 * C, BF), ("sab", 4 * C, BF), ("uu", 4 * C, BF), ("e32", 4 * C, BF),
         ("g32", 4 * C, BF), ("x32", 4 * C, BF), ("omv", C, F32), ("yb", C, F32),
     ]:
@@ -50,7 +51,7 @@ SCRATCH = _scratch()
 POOLS = {"c": 100, "h": 20, "s": 2}
 SEMAPHORES = ([k + str(i) for k in POOLS for i in range(POOLS[k])] + ["sent"]
               + ["ends%d" % t for t in range(ROUNDS)]
-              + ["mean%d_%d" % (t, j) for t in range(ROUNDS) for j in range(2)])
+              + ["mean%d_%d" % (t, j) for t in range(ROUNDS) for j in range(3)])
 
 
 def _mask(engines):
@@ -160,8 +161,8 @@ def rank_program(g, core, T, topo):
         else:
             rec("v", lambda: vec.tensor_scalar(o[0], a[0], val(s1), val(s2), op0, op1), [a, s1, s2], [o], **k)
 
-    def scan(o, d0, d1, first=1.0, **k):
-        rec("v", lambda: vec.tensor_tensor_scan(o[0], d0[0], d1[0], val(first), Op.add, Op.min), [d0, d1, first], [o], **k)
+    def scan(o, d0, d1, first=1.0, op0=Op.add, op1=Op.min, **k):
+        rec("v", lambda: vec.tensor_tensor_scan(o[0], d0[0], d1[0], val(first), op0, op1), [d0, d1, first], [o], **k)
 
     def transp(o, i, **k):
         rec("v", lambda: vec.transpose(o[0], i[0]), [i], [o], **k)
@@ -173,13 +174,13 @@ def rank_program(g, core, T, topo):
         qo, so = A(qn, a, b), A(sn, a, b)
         rec("v", lambda: vec.quantize_mx(qo[0], so[0], i[0]), [i], [qo, so], **k)
 
-    def scal(o, i, scale=None, bias=None, **k):
+    def scal(o, i, scale=None, bias=None, fn=Fn.Identity, **k):
         if scale is None:
             rec("a", lambda: act.activation(o[0], i[0], Fn.Copy), [i], [o], **k)
         elif bias is None:
-            rec("a", lambda: act.activation(o[0], i[0], Fn.Identity, scale=val(scale)), [i, scale], [o], **k)
+            rec("a", lambda: act.activation(o[0], i[0], fn, scale=val(scale)), [i, scale], [o], **k)
         else:
-            rec("a", lambda: act.activation(o[0], i[0], Fn.Identity, bias=val(bias), scale=val(scale)),
+            rec("a", lambda: act.activation(o[0], i[0], fn, bias=val(bias), scale=val(scale)),
                 [i, scale, bias], [o], **k)
 
     def iota(o, pattern, base, cm=0, small=True, **k):
@@ -206,72 +207,91 @@ def rank_program(g, core, T, topo):
         return A(name, C * b + a, C * b + e)
 
     sent = [0]
-    H = CUT[0]
+
+    def runs_of(t):
+        edges = [0] + CUT[t] + [C]
+        return list(zip(edges, edges[1:]))
 
     dma("a", A("ub"), T.u[:])
-    for a, b in ((0, H), (H, C)):
-        dma("y", A("xb0", XO + 4 * a, XO + 4 * b), T.x[:, 4 * a:4 * b])
-    dma("y", bits(A("qw", 0, 512)), T.wc[:], grp="w")
+    for j, (a, b) in enumerate(runs_of(0)):
+        dma("y", A("xb0", XO + 4 * a, XO + 4 * b), T.x[:, 4 * a:4 * b], grp="x%d" % j)
+    dma("y", bits(A("qw", 0, 512)), T.wc[:], grp="w", after=["x%d" % (len(CUT[0]) - 1)])
     dma("y", A("sw", 0, 512), T.ws[:], grp="w")
     dma("y", A("vb"), T.v[:])
 
-    iota(A("uli"), [[16, 8]], 0, small=False)
     iota(A("idm"), [[1, 128]], 0, -1)
-    iota(A("ci", 0, 32), [[0, 4], [1, 8]], 0, grp="ci")
-    iota(A("ci", 32, 64), [[0, 2], [8, 2], [0, 8]], 0, grp="ci")
-    iota(A("ci", 64, 96), [[0, 8], [1, 4]], 4 * 192, grp="ci")
-    iota(A("ci", 96, 112), [[32, 8], [C + 32, 2]], 0, grp="ci")
-    iota(A("ci", 112, 128), [[32, 8], [-C, 2]], C + 16, grp="ci")
+    iota(A("uli"), [[16, 8]], 0, small=False)
+    iota(A("ci", 0, 32), [[0, 2], [8, 2], [0, 8]], 0, grp="ci")
+    iota(A("ci", 128, 160), [[0, 4], [1, 8]], 0, grp="ci")
+    iota(A("ci", 32, 48), [[32, 8], [C + 32, 2]], 0, grp="ci")
+    iota(A("ci", 48, 64), [[32, 8], [-C, 2]], C + 16, grp="ci")
+    iota(A("ci", 64, 96), [[0, 8], [1, 4]], 0, grp="ci")
+    iota(A("ci", 96, 128), [[0, 8], [2, 2], [-1, 2]], 1, grp="ci")
     iota(A("tfi", 0, 400), [[1, 400]], -192)
     iota(A("mi"), [[0, 24], [1, 8]], 0)
-    iota(A("lci"), [[8, 2], [256, 2]], 0)
     iota(A("tki", 0, 400), [[16, 25], [1, 8], [0, 2]], -192)
+    iota(A("lci"), [[8, 2], [256, 2]], 0)
+
+    def unit(k):
+        a = 3 - k if k < 4 else 520
+        quant("qz", "sz", 128 * k, 128 * k + 128, A("z", a, a + 512), grp="units")
 
     fill(A("z"), 0.0)
-    fill(A("hi", 0, C, C - 1), 0.0, grp="fills")
-    fill(A("kb", 0, 16), 0.0, grp="fills")
-    fill(A("kb", C + 16, C + 32), 0.0, grp="fills")
-    fill(A("fq", 0, 4 * C, C), 0.0, grp="fills")
-    copy(A("ul"), A("uli"))
+    for v, n in ((A("hi", 0, C, C - 1), 2), (A("kb", 0, 16), 16), (A("kb", C + 16, C + 32), 16), (A("fq", 0, 4 * C, C), 4)):
+        scal(v, A("idm", 0, n), 0.0, grp="fills")
     ts(A("z", 3, 515, 4), A("idm"), 0.0, 32.0, Op.is_equal, Op.mult)
-    ts(A("z", 523, 1035, 4), A("idm"), 0.0, 0.25, Op.is_equal, Op.mult)
-    for b in range(4):
-        quant("qz", "sz", 128 * b, 128 * b + 128, A("z", 3 - b, 515 - b), grp="z32")
+    ts(A("z", 520, 1032, 4), A("idm"), 0.0, 0.25, Op.is_equal, Op.mult)
+    copy(A("ul"), A("uli"))
+    for k in range(5):
+        unit(k)
     transp(A("ct"), A("ci"))
-    c_q, c_role, c_end, c_f = A("ct", 0, 1), A("ct", 32, 33), A("ct", 64, 65), A("ct", 96, 97)
+    c_role, c_f, c_q = A("ct", 0, 1), A("ct", 32, 33), A("ct", 128, 129)
     c_sign, c_rb, c_om = A("cs", 0, 1), A("cs", 8, 9), A("cs", 16, 17)
     scal(c_sign, c_role, -0.25, 1.0)
     scal(c_rb, c_role, 1.0 / 512)
     scal(c_om, c_role, -0.125, 1.0)
+
+    def score(t, j):
+        a, b = runs_of(t)[j]
+        mm(4 + j, "qup", "sup", 0, "qx%d" % t, "sx%d" % t, a, b)
+        scal(A("pb", a, b), P(4 + j, 0, b - a), c_sign)
+
+    def rises(t, j):
+        a, b = runs_of(t)[j]
+        tt(A("gg", max(a, 1), b), A("pb", max(a, 1), b), A("pb", max(a, 1) - 1, b - 1), Op.is_gt)
+
+    def peaks(t, j):
+        a, b = runs_of(t)[j]
+        h = max(a - 1, 1)
+        tt(A("hi", h, b - 1), A("gg", h, b - 1), A("gg", h + 1, b), Op.is_gt)
+
+    def quant_run(t, j):
+        a, b = runs_of(t)[j]
+        quant("qx%d" % t, "sx%d" % t, a, b, A("xb%d" % t, XO + 4 * a, XO + 4 * b))
+
     quant("qu", "su", 0, 128, A("ub"))
     copy((T.qup[:, 0:128].bitcast(dt.uint32), A("qup")[1]), ind(A("qu", 0, 128), A("ul", 0, 8), word=True))
     scal(A("sup", 0, 128), ind(A("su", 0, 128), A("ul", 0, 8)))
+    scal(A("ce", 0, 2), A("ct", 64, 128, 32), 1.0 / 2048, 768.0 / 2048, grp="ce")
+    scal(A("ce", 3, 1, -1), A("ct", 64, 128, 32), -1.0 / 2048, 771.0 / 2048, grp="ce")
     scal(A("tf"), A("tfi"), 1.0 / 512)
-
-    def score_first(t):
-        mm(4, "qup", "sup", 0, "qx%d" % t, "sx%d" % t, 0, CUT[t])
-        scal(A("pc", 0, CUT[t]), P(4, 0, CUT[t]))
-
-    quant("qx0", "sx0", 0, H, A("xb0", XO, XO + 4 * H))
-    score_first(0)
+    quant_run(0, 0)
+    score(0, 0)
+    quant_run(0, 1)
     ts(A("mm", 0, 192), A("mi"), c_q, None, Op.is_equal, grp="mm")
     ts(A("mm", C - 1, 191, -1), A("mi"), c_q, None, Op.is_equal, grp="mm")
-    quant("qx0", "sx0", H, C, A("xb0", XO + 4 * H, XO + 4 * C))
 
     for t in range(ROUNDS):
         xb, qx, sx = "xb%d" % t, "qx%d" % t, "sx%d" % t
         qn, sn, qe, se, ql, sl, e = ["%s%d" % (k, t) for k in ("qn", "sn", "qe", "se", "ql", "sl", "e")]
         nxb, nqx, nsx = "xb%d" % (t + 1), "qx%d" % (t + 1), "sx%d" % (t + 1)
         last = t == ROUNDS - 1
-        early = t in EARLY
         tag = "r%d" % t
-        H = CUT[t]
-        runs = [(0, CUT[t + 1]), (CUT[t + 1], C)]
+        runs = runs_of(t + 1)
 
-        mm(5, "qup", "sup", 0, qx, sx, H - 2, C)
+        score(t, len(CUT[t]))
         for b in range(4):
             mm(b, "qz", "sz", 128 * b, qx, sx, 0, C)
-        scal(A("pb", H - 2, C), P(5, 0, C - H + 2), c_sign)
         scal(A(xb, XO, XO + 4), A(xb, XO + 4 * C - 4, XO + 4 * C))
         if t == 0:
             scal(A("tk"), A("tki", 1, C + 1), 1.0 / 512, c_rb)
@@ -288,25 +308,29 @@ def rank_program(g, core, T, topo):
             ts(A("la"), A("sel", 7, 192, 8), 512.0, 192.0, Op.mult, Op.add)
             ts(A("lb"), A("sel", C - 1, 191, -8), -512.0, 192.0, Op.mult, Op.add)
 
-        tt(A("df", 1, H), P(4, 1, H), A("pc", 0, H - 1), Op.subtract)
-        ts(A("gg", 1, H), A("df", 1, H), c_sign, 0.0, Op.mult, Op.is_gt)
-        tt(A("hi", 1, H - 1), A("gg", 1, H - 1), A("gg", 2, H), Op.is_gt)
-        tt(A("gg", H, C), A("pb", H, C), A("pb", H - 1, C - 1), Op.is_gt)
-        scan(A("fb", 0, H - 1), A("hi", 0, H - 1), A("tf", 0, H - 1))
-        tt(A("hi", H - 1, C - 1), A("gg", H - 1, C - 1), A("gg", H, C), Op.is_gt)
-        scan(A("fb", H - 1, C), A("hi", H - 1, C), A("tf", H - 1, C), A("fb", H - 2, H - 1))
-        if early:
-            backward()
-        ts(A("eo", 0, 1), A("fb", C - 1, C), 2048.0, c_end, Op.mult, Op.add)
-        if early:
-            choose()
-        copy(A(xb, 0, XO), ind(A(xb, XO, XO + 4 * C), A("eo", 0, 1)))
-        if early:
-            slot_lists()
+        H = CUT[t][0]
+        if t in SPLIT:
+            rises(t, 0)
+            peaks(t, 0)
+            rises(t, 1)
+            scan(A("fb", 0, H - 1), A("hi", 0, H - 1), A("tf", 0, H - 1))
+            peaks(t, 1)
+            scan(A("fb", H - 1, C - 1), A("hi", H - 1, C - 1), A("tf", H - 1, C - 1), A("fb", H - 2, H - 1))
+        else:
+            for j in range(2):
+                rises(t, j)
+            for j in range(2):
+                peaks(t, j)
+            scan(A("fb", 0, C - 1), A("hi", 0, C - 1), A("tf", 0, C - 1))
+        backward()
+        ts(A("eo"), A("ce"), A("fb", C - 2, C - 1), 2048.0, Op.add, Op.mult)
+        scan(A("kb", 16, C + 16), A("hi"), A("tk"))
+        copy(A(xb, 0, XO), ind(A(xb, XO, XO + 4 * C), A("eo")))
+        choose()
         quant(qn, sn, 0, 128, A(xb, 0, 512))
 
         right = T.cores[(rank + 1) % n_ranks]
-        left = T.cores[(rank - 1) % n_ranks]
+        n_end = len(topo.engines(T.cores[(rank - 1) % n_ranks], core))
         eng = topo.engines(core, right)
         rid, pid = topo.addr(right)[:2]
         half = len(eng) // 2
@@ -315,72 +339,84 @@ def rank_program(g, core, T, topo):
             d = DstId(rid=rid, pnc=pid)
             return g.remote_dma_fused([
                 RemoteDMATransfer(dst_ids=[d], dma_engine_mask=_mask(eng[:half]), remote_sem=T.sem["ends%d" % t],
-                                  src=T[qn][:, 0:4].bitcast(dt.uint8), dst=T[qx][:, C:C + 4].bitcast(dt.uint8)),
+                                  src=T[qn][:, 0:16].bitcast(dt.uint8), dst=T[qx][:, C:C + 16].bitcast(dt.uint8)),
                 RemoteDMATransfer(dst_ids=[d], dma_engine_mask=_mask(eng[half:]), remote_sem=T.sem["ends%d" % t],
-                                  src=T[sn][:, 0:16], dst=T[sx][:, C:C + 16]),
+                                  src=T[sn][:, 0:64], dst=T[sx][:, C:C + 64]),
             ], local_sem=T.sem.sent)
 
-        rec("g", send_ends, [A(qn, 0, 4), A(sn, 0, 16)], [])
+        rec("g", send_ends, [A(qn, 0, 16), A(sn, 0, 64)], [])
         sent[0] += len(eng)
 
-        if not early:
-            backward()
-            choose()
-        scan(A("kb", 16, C + 16), A("hi"), A("tk"))
-        if not early:
-            slot_lists()
+        slot_lists()
         transp(A("tr", 0, C), A("kb", 16, C + 16), grp=tag + "tr")
         transp(A("tr", C, 2 * C + 32), A("kb"), grp=tag + "tr")
         if t == 0:
             ts(A("lc"), A("lci"), c_f, float(2 * C + 31), Op.add, Op.min)
-            for b in range(4):
-                quant("qz", "sz", 512 + 128 * b, 640 + 128 * b, A("z", 523 - b, 1035 - b), grp="z4")
-        ts(A("i2"), ind(A("tr"), A("lc")), 512.0, 192.0, Op.mult, Op.add)
-
-        for b in range(4):
-            mm(4 + b, "qz", "sz", 512 + 128 * b, qx, sx, C + 4 - 128, C + 4,
-               ext=[("ends%d" % t, len(topo.engines(left, core)))] if b == 0 else [])
+            quant("qv", "sv", 0, 128, A("vb"))
 
         def slots(b, a, e2):
             tt(win("sab", b, a, e2), ind(win("fq", b), A("lb", a // 16, e2 // 16)), win("tt", b, a, e2), Op.add)
 
         def fix(b):
             v = A("sab", C * b, C * b + 9, 8)
-            tt(v, P(4 + b, 124, 127, 2), v, Op.add)
+            tt(v, P(4, 112 + 4 * b, 115 + 4 * b, 2), v, Op.add)
 
-        for b in range(4):
-            scal(win("tt", b), ind(win("fq", b), A("la")))
-        for b in range(3):
-            slots(b, 0, C)
-        slots(3, 0, 192)
-        if t == 0:
-            quant("qv", "sv", 0, 128, A("vb"))
+        for b, a, e2 in ((0, 0, 128), (0, 128, C), (1, 0, C), (2, 0, C), (3, 0, C)):
+            scal(win("tt", b, a, e2), ind(win("fq", b), A("la", a // 16, e2 // 16)))
+        mm(4, "qz", "sz", 512, qx, sx, C + 16 - 128, C + 16, ext=[("ends%d" % t, n_end)])
+        ts(A("i2"), ind(A("tr"), A("lc")), 512.0, 192.0, Op.mult, Op.add)
+        slots(0, 0, 128)
+        slots(0, 128, C)
+        slots(1, 0, C)
+        slots(2, 0, C)
+        slots(3, 0, PART)
         fix(0)
-        slots(3, 192, C)
-        for b in range(1, 4):
-            fix(b)
+        fix(1)
+        slots(3, PART, C)
+        fix(2)
+        fix(3)
 
         mate = T.cores[rank ^ STEP[t]]
         eng = topo.engines(core, mate)
         rid, pid = topo.addr(mate)[:2]
-        for j, (a, b2) in enumerate(runs):
-            for b in range(4):
-                scal(win("uu", b, a, b2), ind(win("sab", b), A("i2", a // 16, b2 // 16)))
-            for b in range(4):
+
+        def mean(j, planes):
+            a, b2 = runs[j]
+            for b in planes:
                 tt(A(e, 4 * a + b, 4 * b2, 4), ind(win("sab", b), A("i2", 32 + a // 16, 32 + b2 // 16)),
-                   win("uu", b, a, b2), Op.add, grp=tag + "e%d" % j)
+                   win("uu", b, a, b2), Op.add)
+
+        def send_mean(j):
+            a, b2 = runs[j]
             quant(qe, se, a, b2, A(e, 4 * a, 4 * b2))
-            for src, dst in ((A(se, a, b2), A(sl, a, b2)), (bits(A(qe, a, b2)), bits(A(ql, a, b2)))):
+            for src, dst in ((bits(A(qe, a, b2)), bits(A(ql, a, b2))), (A(se, a, b2), A(sl, a, b2))):
                 rec("g", lambda src=src, dst=dst, j=j, t=t, eng=eng, rid=rid, pid=pid: g.remote_dma(
                     dst[0], src[0], T.sem["mean%d_%d" % (t, j)], T.sem.sent, pid, rid, _mask(eng)), [src], [])
                 sent[0] += len(eng)
 
+        def mean32(j, planes):
+            a, b2 = runs[j]
+            for b in planes:
+                scal(win("e32", b, a, b2), A(e, 4 * a + b, 4 * b2, 4), 32.0)
+
+        def rest(j, planes):
+            a, b2 = runs[j]
+            for b in planes:
+                tt(win("g32", b, a, b2), P(b, a, b2), win("e32", b, a, b2), Op.subtract)
+
         for a, b2 in runs:
-            scal(A("e32", 4 * a, 4 * b2), A(e, 4 * a, 4 * b2), 32.0)
-        for j, (a, b2) in enumerate(runs):
             for b in range(4):
-                tt(win("g32", b, a, b2), P(b, a, b2), A("e32", 4 * a + b, 4 * b2, 4), Op.subtract,
-                   grp=tag + "g%d" % j)
+                scal(win("uu", b, a, b2), ind(win("sab", b), A("i2", a // 16, b2 // 16)))
+        mean(0, range(4))
+        mean32(0, range(4))
+        mean(1, [0])
+        send_mean(0)
+        mean(1, [1, 2, 3])
+        mean32(1, range(4))
+        rest(0, [0])
+        send_mean(1)
+        rest(0, [1, 2, 3])
+
         if last:
             scal(A("omv"), A("hi"), c_sign, c_om)
             dma("y", T.om[:], (T.omv[0:128:16, :], A("omv")[1]), grp="om0")
@@ -393,31 +429,37 @@ def rank_program(g, core, T, topo):
             for b in range(4):
                 mm(4 * (1 - j) + b, "qw", "sw", 128 * b, ql, sl, a, b2, ext=need if b == 0 else [])
 
-        def state(j, b):
+        def state(j):
             a, b2 = runs[j]
-            tt(win("x32", b, a, b2), P(4 * (1 - j) + b, 0, b2 - a), win("g32", b, a, b2), Op.add)
-            o, i = A(nxb, XO + 4 * a + b, XO + 4 * b2, 4), win("x32", b, a, b2)
-            if b == 3:
-                ts(o, i, 1.0 / 32, None, Op.mult)
-                quant(nqx, nsx, a, b2, A(nxb, XO + 4 * a, XO + 4 * b2))
-            else:
-                scal(o, i, 1.0 / 32)
+            for b in range(4):
+                tt(win("x32", b, a, b2), P(4 * (1 - j) + b, 0, b2 - a), win("g32", b, a, b2), Op.add)
+                if b < 3:
+                    scal(A(nxb, XO + 4 * a + b, XO + 4 * b2, 4), win("x32", b, a, b2), 1.0 / 32)
 
-        H = CUT[t + 1]
+        def state_last(j):
+            a, b2 = runs[j]
+            ts(A(nxb, XO + 4 * a + 3, XO + 4 * b2, 4), win("x32", 3, a, b2), 1.0 / 32, None, Op.mult)
+
+        H = runs[0][1]
         product(0)
-        for b in range(4):
-            state(0, b)
+        rest(1, range(4))
+        state(0)
+        scal(A(nxb, XO + 3, XO + 4 * H, 4), win("x32", 3, 0, H), 1.0 / 32)
+        product(1)
         if last:
+            quant_run(t + 1, 0)
             mm(4, "qv", "sv", 0, nqx, nsx, 0, H)
             dma("y", T.oc[:, 0:4 * H], bits(A(nqx, 0, H)), grp="outy")
-            scal(A("yb", 0, H), P(4, 0, H))
+            state(1)
+            copy(A("yb", 0, H), P(4, 0, H))
             dma("y", T.y[:, 0:H], A("yb", 0, H), grp="outy")
-        product(1)
-        for b in range(3):
-            state(1, b)
-        if not last:
-            score_first(t + 1)
-        state(1, 3)
+            state_last(1)
+        else:
+            state(1)
+            quant_run(t + 1, 0)
+            state_last(1)
+            score(t + 1, 0)
+        quant_run(t + 1, 1)
         if last:
             mm(5, "qv", "sv", 0, nqx, nsx, H, C)
             dma("y", T.oc[:, 4 * H:4 * C], bits(A(nqx, H, C)), grp="outy")

@@ -4,10 +4,13 @@ from concourse.mybir import dt, AluOpType, ActivationFunctionType
 C = 384
 ROUNDS = 2
 STEP = [1, 2]
-CUT = [[192], [224], [192]]
-SPLIT = [0]
-PART = 96
+CUT = [[128, 256], [224], [224]]
+PLAIN = [(0, 0, 3), (0, 1, 3), (1, 0, 3), (1, 1, 3)]
+HELP = [384, 256]
 XO = 64
+FRONT = 16
+NONE, BOTH = 8, 1
+PS = C + FRONT
 
 X4, U8, BF, F32, I32, U16 = "float8_e4m3fn_x4", "uint8", "bfloat16", "float32", "int32", "uint16"
 
@@ -33,14 +36,15 @@ def _scratch():
     for name, n, d in [
         ("ub", 512, BF), ("qu", 128, X4), ("su", 128, U8), ("qup", 128, X4), ("sup", 128, U8),
         ("vb", 512, BF), ("qv", 128, X4), ("sv", 128, U8), ("qw", 512, X4), ("sw", 512, U8),
-        ("idm", 128, F32), ("z", 1040, BF), ("qz", 640, X4), ("sz", 640, U8),
-        ("uli", 8, I32), ("ul", 8, U16), ("ci", 160, F32), ("ct", 160, F32), ("cs", 24, F32), ("ce", 4, F32),
-        ("tfi", 400, BF), ("tf", 400, BF), ("tki", 400, BF), ("tk", C, BF), ("mi", 192, BF), ("mm", C, BF),
-        ("lci", 4, F32), ("lc", 4, U16),
-        ("pc", C, F32), ("df", C, BF), ("gg", C, BF), ("pb", C, F32), ("hi", C, BF), ("fb", 2 * C, BF), ("sel", C, BF),
-        ("kb", C + 32, BF), ("tr", 2 * C + 32, BF), ("la", 24, U16), ("lb", 24, U16), ("i2", 64, U16), ("eo", 4, U16),
-        ("fq", 4 * C, BF), ("tt", 4 * C, BF), ("sab", 4 * C, BF), ("uu", 4 * C, BF), ("e32", 4 * C, BF),
-        ("g32", 4 * C, BF), ("x32", 4 * C, BF), ("omv", C, F32), ("yb", C, F32),
+        ("idm", 128, F32), ("z", 1040, BF), ("qz", 1024, X4), ("sz", 1024, U8),
+        ("uli", 8, I32), ("ul", 8, U16), ("ci", 96, F32), ("ct", 96, F32), ("cs", 24, F32),
+        ("tfi", 400, BF), ("tf", 400, BF), ("tki", 400, BF), ("tk", C, BF), ("mi", 192, BF), ("mm", 192, BF),
+        ("lci", 4, F32), ("lc", 4, U16), ("cei", 4, F32), ("ce", 4, F32),
+        ("gg", C, BF), ("pb", C, F32), ("hi", C, BF), ("fb", 2 * C, BF), ("sel", 192, BF), ("lf", 192, F32),
+        ("kb", C + 32, BF), ("tr", 2 * C + 32, BF), ("lb", 24, U16), ("i2", 64, U16), ("eo", 8, U16),
+        ("fq", 4 * C, BF), ("nx", 4 * C, BF), ("ts", 4 * PS, BF), ("uu", 4 * C, BF), ("vv", 4 * C, BF),
+        ("e32", 4 * C, BF),
+        ("g32", 4 * C, BF), ("x32", 4 * C, BF), ("oh", 64, BF), ("od", 24, BF), ("omv", 24, F32), ("yb", C, F32),
     ]:
         sb(name, n, d)
     s["ps"] = ("psum", [128, 4096], F32)
@@ -214,72 +218,72 @@ def rank_program(g, core, T, topo):
 
     dma("a", A("ub"), T.u[:])
     for j, (a, b) in enumerate(runs_of(0)):
-        dma("y", A("xb0", XO + 4 * a, XO + 4 * b), T.x[:, 4 * a:4 * b], grp="x%d" % j)
-    dma("y", bits(A("qw", 0, 512)), T.wc[:], grp="w", after=["x%d" % (len(CUT[0]) - 1)])
+        dma("ya"[j % 2], A("xb0", XO + 4 * a, XO + 4 * b), T.x[:, 4 * a:4 * b], grp="x%d" % j)
+    dma("y", bits(A("qw", 0, 512)), T.wc[:], grp="w", after=["x%d" % len(CUT[0])])
     dma("y", A("sw", 0, 512), T.ws[:], grp="w")
-    dma("y", A("vb"), T.v[:])
 
     iota(A("idm"), [[1, 128]], 0, -1)
     iota(A("uli"), [[16, 8]], 0, small=False)
-    iota(A("ci", 0, 32), [[0, 2], [8, 2], [0, 8]], 0, grp="ci")
-    iota(A("ci", 128, 160), [[0, 4], [1, 8]], 0, grp="ci")
+    iota(A("ci", 0, 32), [[0, 16], [1, 2]], 0, grp="ci")
+    iota(A("ci", 64, 96), [[0, 2], [1, 8], [0, 2]], 0, grp="ci")
     iota(A("ci", 32, 48), [[32, 8], [C + 32, 2]], 0, grp="ci")
     iota(A("ci", 48, 64), [[32, 8], [-C, 2]], C + 16, grp="ci")
-    iota(A("ci", 64, 96), [[0, 8], [1, 4]], 0, grp="ci")
-    iota(A("ci", 96, 128), [[0, 8], [2, 2], [-1, 2]], 1, grp="ci")
+    iota(A("cei"), [[1, 4]], 4 * 192)
     iota(A("tfi", 0, 400), [[1, 400]], -192)
-    iota(A("mi"), [[0, 24], [1, 8]], 0)
-    iota(A("tki", 0, 400), [[16, 25], [1, 8], [0, 2]], -192)
-    iota(A("lci"), [[8, 2], [256, 2]], 0)
+    iota(A("mi"), [[0, 24], [-1, 8]], 7)
+    iota(A("tki", 0, 400), [[2, 200], [0, 2]], FRONT - 200)
+    iota(A("lci"), [[1, 2], [256, 2]], 0)
 
     def unit(k):
-        a = 3 - k if k < 4 else 520
-        quant("qz", "sz", 128 * k, 128 * k + 128, A("z", a, a + 512), grp="units")
+        a = 3 - k if k < 4 else 527 - k
+        quant("qz", "sz", 128 * k, 128 * k + 128, A("z", a, a + 512), grp="units%d" % (k // 4))
 
     fill(A("z"), 0.0)
-    for v, n in ((A("hi", 0, C, C - 1), 2), (A("kb", 0, 16), 16), (A("kb", C + 16, C + 32), 16), (A("fq", 0, 4 * C, C), 4)):
+    zeros = [(A("hi", 0, C, C - 1), 2), (A("kb", 0, 16), 16), (A("kb", C + 16, C + 32), 16), (A("fq", 0, 4 * C, C), 4)]
+    for v, n in zeros + [(A("ts", PS * b, PS * b + FRONT + 2), FRONT + 2) for b in range(4)]:
         scal(v, A("idm", 0, n), 0.0, grp="fills")
     ts(A("z", 3, 515, 4), A("idm"), 0.0, 32.0, Op.is_equal, Op.mult)
-    ts(A("z", 520, 1032, 4), A("idm"), 0.0, 0.25, Op.is_equal, Op.mult)
+    ts(A("z", 523, 1035, 4), A("idm"), 0.0, 0.25, Op.is_equal, Op.mult)
     copy(A("ul"), A("uli"))
-    for k in range(5):
+    for k in range(6):
         unit(k)
     transp(A("ct"), A("ci"))
-    c_role, c_f, c_q = A("ct", 0, 1), A("ct", 32, 33), A("ct", 128, 129)
-    c_sign, c_rb, c_om = A("cs", 0, 1), A("cs", 8, 9), A("cs", 16, 17)
-    scal(c_sign, c_role, -0.25, 1.0)
+    quant("qu", "su", 0, 128, A("ub"))
+    copy((T.qup[:, 0:128].bitcast(dt.uint32), A("qup")[1]), ind(A("qu", 0, 128), A("ul", 0, 8), word=True))
+    scal(A("sup", 0, 128), ind(A("su", 0, 128), A("ul", 0, 8)))
+    c_role, c_f, c_q = A("ct", 0, 1), A("ct", 32, 33), A("ct", 64, 65)
+    c_sign, c_rb, c_none = A("cs", 0, 1), A("cs", 8, 9), A("cs", 16, 17)
+    scal(c_sign, c_role, -2.0, 1.0)
+    scal(A("ce"), A("cei"), 1.0 / 2048)
     scal(c_rb, c_role, 1.0 / 512)
-    scal(c_om, c_role, -0.125, 1.0)
+    scal(c_none, c_role, 1.0 / 512, (NONE - 200) / 512)
 
     def score(t, j):
         a, b = runs_of(t)[j]
-        mm(4 + j, "qup", "sup", 0, "qx%d" % t, "sx%d" % t, a, b)
-        scal(A("pb", a, b), P(4 + j, 0, b - a), c_sign)
+        bank = (4, 5)[j] if len(CUT[t]) == 1 else (0, 1, 5)[j]
+        mm(bank, "qup", "sup", 0, "qx%d" % t, "sx%d" % t, a, b)
+        scal(A("pb", a, b), P(bank, 0, b - a), c_sign)
 
     def rises(t, j):
         a, b = runs_of(t)[j]
         tt(A("gg", max(a, 1), b), A("pb", max(a, 1), b), A("pb", max(a, 1) - 1, b - 1), Op.is_gt)
 
-    def peaks(t, j):
-        a, b = runs_of(t)[j]
-        h = max(a - 1, 1)
-        tt(A("hi", h, b - 1), A("gg", h, b - 1), A("gg", h + 1, b), Op.is_gt)
+    def peaks(a, b):
+        tt(A("hi", a, b), A("gg", a, b), A("gg", a + 1, b + 1), Op.is_gt)
 
     def quant_run(t, j):
         a, b = runs_of(t)[j]
         quant("qx%d" % t, "sx%d" % t, a, b, A("xb%d" % t, XO + 4 * a, XO + 4 * b))
 
-    quant("qu", "su", 0, 128, A("ub"))
-    copy((T.qup[:, 0:128].bitcast(dt.uint32), A("qup")[1]), ind(A("qu", 0, 128), A("ul", 0, 8), word=True))
-    scal(A("sup", 0, 128), ind(A("su", 0, 128), A("ul", 0, 8)))
-    scal(A("ce", 0, 2), A("ct", 64, 128, 32), 1.0 / 2048, 768.0 / 2048, grp="ce")
-    scal(A("ce", 3, 1, -1), A("ct", 64, 128, 32), -1.0 / 2048, 771.0 / 2048, grp="ce")
     scal(A("tf"), A("tfi"), 1.0 / 512)
     quant_run(0, 0)
     score(0, 0)
     quant_run(0, 1)
-    ts(A("mm", 0, 192), A("mi"), c_q, None, Op.is_equal, grp="mm")
-    ts(A("mm", C - 1, 191, -1), A("mi"), c_q, None, Op.is_equal, grp="mm")
+    score(0, 1)
+    ts(A("mm"), A("mi"), c_q, None, Op.is_equal)
+    unit(6)
+    quant_run(0, 2)
+    unit(7)
 
     for t in range(ROUNDS):
         xb, qx, sx = "xb%d" % t, "qx%d" % t, "sx%d" % t
@@ -295,38 +299,31 @@ def rank_program(g, core, T, topo):
         scal(A(xb, XO, XO + 4), A(xb, XO + 4 * C - 4, XO + 4 * C))
         if t == 0:
             scal(A("tk"), A("tki", 1, C + 1), 1.0 / 512, c_rb)
-        for b in range(4):
+        ahead = 3 if t == 0 else 4
+        for b in range(ahead):
             scal(win("fq", b, 1), P(b, 1, C), 1.0 / 128)
 
-        def backward():
-            scan(A("fb", C, 2 * C), A("hi", None, None, -1), A("tf", 1, C + 1))
-
-        def choose():
-            scan(A("sel"), A("mm"), A("fb", 0, 2 * C, 2))
-
-        def slot_lists():
-            ts(A("la"), A("sel", 7, 192, 8), 512.0, 192.0, Op.mult, Op.add)
-            ts(A("lb"), A("sel", C - 1, 191, -8), -512.0, 192.0, Op.mult, Op.add)
-
-        H = CUT[t][0]
-        if t in SPLIT:
-            rises(t, 0)
-            peaks(t, 0)
-            rises(t, 1)
-            scan(A("fb", 0, H - 1), A("hi", 0, H - 1), A("tf", 0, H - 1))
-            peaks(t, 1)
-            scan(A("fb", H - 1, C - 1), A("hi", H - 1, C - 1), A("tf", H - 1, C - 1), A("fb", H - 2, H - 1))
-        else:
-            for j in range(2):
-                rises(t, j)
-            for j in range(2):
-                peaks(t, j)
-            scan(A("fb", 0, C - 1), A("hi", 0, C - 1), A("tf", 0, C - 1))
-        backward()
-        ts(A("eo"), A("ce"), A("fb", C - 2, C - 1), 2048.0, Op.add, Op.mult)
-        scan(A("kb", 16, C + 16), A("hi"), A("tk"))
-        copy(A(xb, 0, XO), ind(A(xb, XO, XO + 4 * C), A("eo")))
-        choose()
+        H = CUT[t][-1]
+        for j in range(len(CUT[t]) + 1):
+            rises(t, j)
+        peaks(1, H - 1)
+        peaks(H - 1, C - 1)
+        if last:
+            for k in range(2):
+                dma("y", A("oh", 32 * k, 32 * k + 24), (T.hi[k:128:16, :], A("hi")[1]), grp="oh")
+        if t == 0:
+            ts(A("lc"), A("lci"), c_f, float(2 * C + 31), Op.add, Op.min)
+        scan(A("fb", 0, C - 1), A("hi", 0, C - 1), A("tf", 0, C - 1))
+        scan(A("fb", C, 2 * C), A("hi", None, None, -1), A("tf", 1, C + 1))
+        ts(A("eo", 0, 8, 2), A("ce"), A("fb", C - 2, C - 1), 2048.0, Op.add, Op.mult)
+        scan(A("kb", 16, C + 16), A("hi"), A("tk"), c_none)
+        scan(A("sel"), A("mm"), A("fb", C, 2 * C, 2))
+        for c in range(4):
+            (copy if c < 2 else scal)(A(xb, c, XO, 4), ind(A(xb, XO, XO + 4 * C), A("eo", 2 * c, 2 * c + 1)),
+                                      grp=tag + "en")
+        for b in range(ahead, 4):
+            scal(win("fq", b, 1), P(b, 1, C), 1.0 / 128)
+        ts(A("lb"), A("sel", 191, None, -8), -512.0, 192.0, Op.mult, Op.add)
         quant(qn, sn, 0, 128, A(xb, 0, 512))
 
         right = T.cores[(rank + 1) % n_ranks]
@@ -339,52 +336,66 @@ def rank_program(g, core, T, topo):
             d = DstId(rid=rid, pnc=pid)
             return g.remote_dma_fused([
                 RemoteDMATransfer(dst_ids=[d], dma_engine_mask=_mask(eng[:half]), remote_sem=T.sem["ends%d" % t],
-                                  src=T[qn][:, 0:16].bitcast(dt.uint8), dst=T[qx][:, C:C + 16].bitcast(dt.uint8)),
+                                  src=T[qn][:, 0:4].bitcast(dt.uint8), dst=T[qx][:, C:C + 4].bitcast(dt.uint8)),
                 RemoteDMATransfer(dst_ids=[d], dma_engine_mask=_mask(eng[half:]), remote_sem=T.sem["ends%d" % t],
-                                  src=T[sn][:, 0:64], dst=T[sx][:, C:C + 64]),
+                                  src=T[sn][:, 0:16], dst=T[sx][:, C:C + 16]),
             ], local_sem=T.sem.sent)
 
-        rec("g", send_ends, [A(qn, 0, 16), A(sn, 0, 64)], [])
+        rec("g", send_ends, [A(qn, 0, 4), A(sn, 0, 16)], [])
         sent[0] += len(eng)
 
-        slot_lists()
+        top = C - HELP[t]
+        for b in range(3):
+            scal(win("nx", b), ind(win("fq", b), A("lb")))
+        if top:
+            scal(win("nx", 3, 0, top), ind(win("fq", 3), A("lb", 0, top // 16)))
+        for b in range(4):
+            mm(4 + b, "qz", "sz", 512 + 128 * b, qx, sx, C + 4 - 128, C + 4,
+               ext=[("ends%d" % t, n_end)] if b == 0 else [])
+
+        def pairs(b):
+            tt(A("ts", PS * b + FRONT + 2, PS * b + PS), win("nx", b, 0, C - 2), win("nx", b, 2, C), Op.add)
+
+        ia, ic, most, least, down, low = [A("lf", a, a + 24) for a in (0, 32, 64, 96, 128, 160)]
         transp(A("tr", 0, C), A("kb", 16, C + 16), grp=tag + "tr")
         transp(A("tr", C, 2 * C + 32), A("kb"), grp=tag + "tr")
+        copy(win("nx", 3, top, C), ind(win("fq", 3), A("lb", top // 16, C // 16)))
+        ts(A("lf", 0, 64), ind(A("tr"), A("lc")), 512.0, 200.0, Op.mult, Op.add)
+        pairs(0)
+        tt(most, ia, ic, Op.max)
+        tt(least, ia, ic, Op.min)
+        pairs(1)
+        ts(A("i2", 0, 24), most, float(FRONT), float(FRONT), Op.max, Op.subtract)
+        ts(down, most, float(FRONT), float(BOTH - NONE), Op.is_lt, Op.mult)
+        pairs(2)
+        tt(low, least, down, Op.add)
+        pairs(3)
+        copy(A("i2", 32, 56), low)
+
+        if last:
+            tt(A("od"), A("oh", 0, 24), A("oh", 32, 56), Op.subtract)
+
+        for b in range(4):
+            tt(A("ts", PS * b + NONE, PS * b + NONE + 2), P(4 + b, 124, 126), win("nx", b, 0, 2), Op.add)
+        for b in range(4):
+            tt(A("ts", PS * b + BOTH, PS * b + BOTH + 1), A("ts", PS * b + NONE, PS * b + NONE + 1),
+               A("ts", PS * b + NONE + 1, PS * b + NONE + 2), Op.add)
+
         if t == 0:
-            ts(A("lc"), A("lci"), c_f, float(2 * C + 31), Op.add, Op.min)
-            quant("qv", "sv", 0, 128, A("vb"))
-
-        def slots(b, a, e2):
-            tt(win("sab", b, a, e2), ind(win("fq", b), A("lb", a // 16, e2 // 16)), win("tt", b, a, e2), Op.add)
-
-        def fix(b):
-            v = A("sab", C * b, C * b + 9, 8)
-            tt(v, P(4, 112 + 4 * b, 115 + 4 * b, 2), v, Op.add)
-
-        for b, a, e2 in ((0, 0, 128), (0, 128, C), (1, 0, C), (2, 0, C), (3, 0, C)):
-            scal(win("tt", b, a, e2), ind(win("fq", b), A("la", a // 16, e2 // 16)))
-        mm(4, "qz", "sz", 512, qx, sx, C + 16 - 128, C + 16, ext=[("ends%d" % t, n_end)])
-        ts(A("i2"), ind(A("tr"), A("lc")), 512.0, 192.0, Op.mult, Op.add)
-        slots(0, 0, 128)
-        slots(0, 128, C)
-        slots(1, 0, C)
-        slots(2, 0, C)
-        slots(3, 0, PART)
-        fix(0)
-        fix(1)
-        slots(3, PART, C)
-        fix(2)
-        fix(3)
+            dma("y", A("vb"), (T.v[:], A("ts", BOTH, BOTH + 1)[1]))
 
         mate = T.cores[rank ^ STEP[t]]
         eng = topo.engines(core, mate)
         rid, pid = topo.addr(mate)[:2]
 
+        def second(j, b):
+            a, b2 = runs[j]
+            return ind(A("ts", PS * b, PS * b + PS), A("i2", 32 + a // 16, 32 + b2 // 16))
+
         def mean(j, planes):
             a, b2 = runs[j]
             for b in planes:
-                tt(A(e, 4 * a + b, 4 * b2, 4), ind(win("sab", b), A("i2", 32 + a // 16, 32 + b2 // 16)),
-                   win("uu", b, a, b2), Op.add)
+                tt(A(e, 4 * a + b, 4 * b2, 4), win("vv", b, a, b2) if (t, j, b) in PLAIN else second(j, b), win("uu", b, a, b2), Op.add)
 
         def send_mean(j):
             a, b2 = runs[j]
@@ -394,9 +405,9 @@ def rank_program(g, core, T, topo):
                     dst[0], src[0], T.sem["mean%d_%d" % (t, j)], T.sem.sent, pid, rid, _mask(eng)), [src], [])
                 sent[0] += len(eng)
 
-        def mean32(j, planes):
+        def mean32(j):
             a, b2 = runs[j]
-            for b in planes:
+            for b in range(4):
                 scal(win("e32", b, a, b2), A(e, 4 * a + b, 4 * b2, 4), 32.0)
 
         def rest(j, planes):
@@ -404,72 +415,77 @@ def rank_program(g, core, T, topo):
             for b in planes:
                 tt(win("g32", b, a, b2), P(b, a, b2), win("e32", b, a, b2), Op.subtract)
 
-        for a, b2 in runs:
+        for j, (a, b2) in enumerate(runs):
             for b in range(4):
-                scal(win("uu", b, a, b2), ind(win("sab", b), A("i2", a // 16, b2 // 16)))
+                scal(win("uu", b, a, b2), ind(A("ts", PS * b + FRONT, PS * b + PS), A("i2", a // 16, b2 // 16)))
+                if last and a == 0 and b == 2:
+                    scal(A("omv"), A("od"), 1.0, 1.0)
+                    dma("y", T.om[:], A("omv"), grp="outy")
+            if (t, j, 3) in PLAIN:
+                scal(win("vv", 3, a, b2), second(j, 3))
+        n = len(runs) - 1
         mean(0, range(4))
-        mean32(0, range(4))
-        mean(1, [0])
-        send_mean(0)
-        mean(1, [1, 2, 3])
-        mean32(1, range(4))
+        for j in range(n):
+            mean32(j)
+            mean(j + 1, [0])
+            send_mean(j)
+            mean(j + 1, [1, 2, 3])
+        mean32(n)
         rest(0, [0])
-        send_mean(1)
+        send_mean(n)
         rest(0, [1, 2, 3])
-
-        if last:
-            scal(A("omv"), A("hi"), c_sign, c_om)
-            dma("y", T.om[:], (T.omv[0:128:16, :], A("omv")[1]), grp="om0")
-            rec("g", lambda: g.dma_start(T.om[:], T.omv[8:128:16, :], accum_op=Op.add), [A("omv")], [], grp="om1",
-                pool="s", inc=16, after=["om0"])
 
         def product(j):
             a, b2 = runs[j]
             need = [("mean%d_%d" % (t, j), 2 * len(topo.engines(mate, core)))]
             for b in range(4):
-                mm(4 * (1 - j) + b, "qw", "sw", 128 * b, ql, sl, a, b2, ext=need if b == 0 else [])
+                mm(4 * (1 - j % 2) + b, "qw", "sw", 128 * b, ql, sl, a, b2, ext=need if b == 0 else [])
 
         def state(j):
             a, b2 = runs[j]
             for b in range(4):
-                tt(win("x32", b, a, b2), P(4 * (1 - j) + b, 0, b2 - a), win("g32", b, a, b2), Op.add)
-                if b < 3:
+                tt(win("x32", b, a, b2), P(4 * (1 - j % 2) + b, 0, b2 - a), win("g32", b, a, b2), Op.add)
+                if b < 3 or j < n:
                     scal(A(nxb, XO + 4 * a + b, XO + 4 * b2, 4), win("x32", b, a, b2), 1.0 / 32)
 
-        def state_last(j):
-            a, b2 = runs[j]
+        def state_last():
+            a, b2 = runs[n]
             ts(A(nxb, XO + 4 * a + 3, XO + 4 * b2, 4), win("x32", 3, a, b2), 1.0 / 32, None, Op.mult)
 
-        H = runs[0][1]
+        H = runs[n][0]
         product(0)
-        rest(1, range(4))
-        state(0)
-        scal(A(nxb, XO + 3, XO + 4 * H, 4), win("x32", 3, 0, H), 1.0 / 32)
-        product(1)
         if last:
+            rest(1, range(4))
+            state(0)
+            product(1)
+            state(1)
             quant_run(t + 1, 0)
             mm(4, "qv", "sv", 0, nqx, nsx, 0, H)
             dma("y", T.oc[:, 0:4 * H], bits(A(nqx, 0, H)), grp="outy")
-            state(1)
-            copy(A("yb", 0, H), P(4, 0, H))
-            dma("y", T.y[:, 0:H], A("yb", 0, H), grp="outy")
-            state_last(1)
+            state_last()
+            scal(A("yb", 0, H), P(4, 0, H))
         else:
+            rest(1, range(4))
+            state(0)
+            product(1)
             state(1)
             quant_run(t + 1, 0)
-            state_last(1)
+            state_last()
             score(t + 1, 0)
-        quant_run(t + 1, 1)
+        quant_run(t + 1, n)
+        if t == 0:
+            quant("qv", "sv", 0, 128, A("vb"))
         if last:
             mm(5, "qv", "sv", 0, nqx, nsx, H, C)
             dma("y", T.oc[:, 4 * H:4 * C], bits(A(nqx, H, C)), grp="outy")
             for k in range(4):
                 dma("y" if k < 2 else "a", T.osc[4 * k:4 * k + 4, 0:C],
                     (T[nsx][32 * k:32 * k + 4, 0:C], A(nsx, 0, C)[1]), grp="outy" if k < 2 else "outa")
+            dma("y", T.y[:, 0:H], A("yb", 0, H), grp="outy")
             copy(A("yb", H, C), P(5, 0, C - H))
             dma("a", T.y[:, H:C], A("yb", H, C), grp="outa")
 
     rec("y", None, [], [], after=["outy"])
     rec("a", None, [], [], after=["outa"])
-    rec("g", None, [], [], after=["om1"], ext=[("sent", sent[0])])
+    rec("g", None, [], [], ext=[("sent", sent[0])])
     emit(ops, queues, T)

from concourse.bass import DstId, RemoteDMATransfer
from concourse.mybir import dt, AluOpType, ActivationFunctionType

C = 384
ROUNDS = 2
STEP = [1, 2]
CUT = [[128, 256], [224], [224]]
PLAIN = [(0, 0, 3), (0, 1, 3), (1, 0, 3), (1, 1, 3)]
HELP = [384, 256]
XO = 64
FRONT = 16
NONE, BOTH = 8, 1
PS = C + FRONT

X4, U8, BF, F32, I32, U16 = "float8_e4m3fn_x4", "uint8", "bfloat16", "float32", "int32", "uint16"


def _scratch():
    s = {}

    def sb(name, n, d):
        s[name] = ("sbuf", [128, n], d)

    for t in range(ROUNDS + 1):
        sb("xb%d" % t, XO + 4 * C, BF)
        sb("qx%d" % t, C + 16, X4)
        sb("sx%d" % t, C + 64, U8)
    for t in range(ROUNDS):
        sb("qn%d" % t, 128, X4)
        sb("sn%d" % t, 128, U8)
        sb("qe%d" % t, C, X4)
        sb("se%d" % t, C, U8)
        sb("ql%d" % t, C, X4)
        sb("sl%d" % t, C, U8)
        sb("e%d" % t, 4 * C, BF)
    for name, n, d in [
        ("ub", 512, BF), ("qu", 128, X4), ("su", 128, U8), ("qup", 128, X4), ("sup", 128, U8),
        ("vb", 512, BF), ("qv", 128, X4), ("sv", 128, U8), ("qw", 512, X4), ("sw", 512, U8),
        ("idm", 128, F32), ("z", 1040, BF), ("qz", 1024, X4), ("sz", 1024, U8),
        ("uli", 8, I32), ("ul", 8, U16), ("ci", 96, F32), ("ct", 96, F32), ("cs", 24, F32),
        ("tfi", 400, BF), ("tf", 400, BF), ("tki", 400, BF), ("tk", C, BF), ("mi", 192, BF), ("mm", 192, BF),
        ("lci", 4, F32), ("lc", 4, U16), ("cei", 4, F32), ("ce", 4, F32),
        ("gg", C, BF), ("pb", C, F32), ("hi", C, BF), ("fb", 2 * C, BF), ("sel", 192, BF), ("lf", 192, F32),
        ("kb", C + 32, BF), ("tr", 2 * C + 32, BF), ("lb", 24, U16), ("i2", 64, U16), ("eo", 8, U16),
        ("fq", 4 * C, BF), ("nx", 4 * C, BF), ("ts", 4 * PS, BF), ("uu", 4 * C, BF), ("vv", 4 * C, BF),
        ("e32", 4 * C, BF),
        ("g32", 4 * C, BF), ("x32", 4 * C, BF), ("oh", 64, BF), ("od", 24, BF), ("omv", 24, F32), ("yb", C, F32),
    ]:
        sb(name, n, d)
    s["ps"] = ("psum", [128, 4096], F32)
    return s


SCRATCH = _scratch()
POOLS = {"c": 100, "h": 20, "s": 2}
SEMAPHORES = ([k + str(i) for k in POOLS for i in range(POOLS[k])] + ["sent"]
              + ["ends%d" % t for t in range(ROUNDS)]
              + ["mean%d_%d" % (t, j) for t in range(ROUNDS) for j in range(3)])


def _mask(engines):
    return sum(1 << e for e in engines)


def emit(ops, queues, T):
    groups = {}
    for i, o in enumerate(ops):
        groups.setdefault(o["grp"], []).append(i)
    known = {q: set() for q in queues}
    for i, o in enumerate(ops):
        deps = set()
        for j in range(i):
            p = ops[j]
            hit = False
            for name, m in o["w"].items():
                hit = hit or bool(m & (p["w"].get(name, 0) | p["r"].get(name, 0)))
            for name, m in o["r"].items():
                hit = hit or bool(m & p["w"].get(name, 0))
                if name == "ps" and p["q"] != o["q"]:
                    hit = hit or bool(m & p["r"].get(name, 0))
            if hit or p["grp"] in o["after"]:
                deps.add(j)
        k = known[o["q"]]
        waits = []
        for j in sorted(deps, reverse=True):
            if j in k:
                continue
            members = groups[ops[j]["grp"]]
            assert max(members) < i, (o["grp"], ops[j]["grp"])
            waits.append(ops[j]["grp"])
            for m in members:
                k.add(m)
                k |= ops[m]["known"]
        o["waits"] = waits
        o["known"] = set(k)
    needed = set(w for o in ops for w in o["waits"])
    last, count, where = {}, {}, {}
    for key, members in groups.items():
        if key not in needed:
            continue
        pool = ops[members[0]]["pool"]
        for n in range(POOLS[pool]):
            name = pool + str(n)
            if all(a in ops[m]["known"] for m in members for a in last.get(name, [])):
                break
        else:
            raise ValueError("out of semaphores")
        last[name] = members
        count[name] = count.get(name, 0) + sum(ops[m]["inc"] for m in members)
        where[key] = (name, count[name])
    for o in ops:
        q = queues[o["q"]]
        for name, val in [where[w] for w in o["waits"]] + o["ext"]:
            q.wait_ge(T.sem[name], val)
        if o["fn"] is not None:
            ins = o["fn"]()
            if o["grp"] in where:
                ins.then_inc(T.sem[where[o["grp"]][0]], o["inc"])


def rank_program(g, core, T, topo):
    rank = T.rank_of(core)
    if rank is None:
        return
    n_ranks = len(T.cores)
    vec, act, pe = g.vector, g.scalar, g.tensor
    queues = {"g": g, "v": vec, "a": act, "p": pe, "y": g.sync}
    Op, Fn = AluOpType, ActivationFunctionType
    ops = []

    def A(name, a=None, b=None, s=None):
        cols = range(*slice(a, b, s).indices(SCRATCH[name][1][1]))
        m = 0
        for c in cols:
            m |= 1 << (c // 512 if name == "ps" else c)
        ap = T[name][:, a:b] if s is None else T[name][:, a:b:s]
        return (ap, [(name, m)])

    def ind(win, off, word=False):
        ap = win[0].bitcast(dt.uint32) if word else win[0]
        return (ap.indirect(off[0]), win[1] + off[1])

    def rec(q, fn, r, w, grp=None, pool="c", inc=1, ext=(), after=()):
        rd, wr = {}, {}
        for d, views in ((rd, r), (wr, w)):
            for v in views:
                if isinstance(v, tuple):
                    for name, m in v[1]:
                        d[name] = d.get(name, 0) | m
        ops.append({"q": q, "fn": fn, "r": rd, "w": wr, "grp": grp if grp else "op%d" % len(ops), "pool": pool,
                    "inc": inc, "ext": list(ext), "after": list(after)})

    def val(s):
        return s[0] if isinstance(s, tuple) else s

    def copy(o, i, **k):
        rec("v", lambda: vec.tensor_copy(o[0], i[0]), [i], [o], **k)

    def tt(o, a, b, op, **k):
        rec("v", lambda: vec.tensor_tensor(o[0], a[0], b[0], op), [a, b], [o], **k)

    def ts(o, a, s1, s2, op0, op1=None, **k):
        if op1 is None:
            rec("v", lambda: vec.tensor_scalar(o[0], a[0], val(s1), None, op0), [a, s1], [o], **k)
        else:
            rec("v", lambda: vec.tensor_scalar(o[0], a[0], val(s1), val(s2), op0, op1), [a, s1, s2], [o], **k)

    def scan(o, d0, d1, first=1.0, op0=Op.add, op1=Op.min, **k):
        rec("v", lambda: vec.tensor_tensor_scan(o[0], d0[0], d1[0], val(first), op0, op1), [d0, d1, first], [o], **k)

    def transp(o, i, **k):
        rec("v", lambda: vec.transpose(o[0], i[0]), [i], [o], **k)

    def fill(o, c, **k):
        rec("v", lambda: vec.memset(o[0], c), [], [o], **k)

    def quant(qn, sn, a, b, i, **k):
        qo, so = A(qn, a, b), A(sn, a, b)
        rec("v", lambda: vec.quantize_mx(qo[0], so[0], i[0]), [i], [qo, so], **k)

    def scal(o, i, scale=None, bias=None, fn=Fn.Identity, **k):
        if scale is None:
            rec("a", lambda: act.activation(o[0], i[0], Fn.Copy), [i], [o], **k)
        elif bias is None:
            rec("a", lambda: act.activation(o[0], i[0], fn, scale=val(scale)), [i, scale], [o], **k)
        else:
            rec("a", lambda: act.activation(o[0], i[0], fn, bias=val(bias), scale=val(scale)),
                [i, scale, bias], [o], **k)

    def iota(o, pattern, base, cm=0, small=True, **k):
        if small:
            rec("g", lambda: g.iota(o[0], pattern, base, cm, allow_small_or_imprecise_dtypes=True), [], [o], **k)
        else:
            rec("g", lambda: g.iota(o[0], pattern, base, cm), [], [o], **k)

    def mm(bank, wq, ws, w0, xq, xs, a, b, **k):
        o = A("ps", 512 * bank, 512 * bank + b - a)
        l, ls, r, rs = A(wq, w0, w0 + 128), A(ws, w0, w0 + 128), A(xq, a, b), A(xs, a, b)
        rec("p", lambda: pe.matmul_mx(o[0], l[0], ls[0], r[0], rs[0], True, True), [l, ls, r, rs], [o], **k)

    def dma(q, o, i, **k):
        rec(q, lambda: queues[q].dma_start(val(o), val(i)), [i], [o], pool="h", inc=16, **k)

    def bits(v):
        return (v[0].bitcast(dt.uint8), v[1])

    def P(bank, a, b, s=None):
        return A("ps", 512 * bank + a, 512 * bank + b, s)

    def win(name, b, a=0, e=C):
        return A(name, C * b + a, C * b + e)

    sent = [0]

    def runs_of(t):
        edges = [0] + CUT[t] + [C]
        return list(zip(edges, edges[1:]))

    dma("a", A("ub"), T.u[:])
    for j, (a, b) in enumerate(runs_of(0)):
        dma("ya"[j % 2], A("xb0", XO + 4 * a, XO + 4 * b), T.x[:, 4 * a:4 * b], grp="x%d" % j)
    dma("y", bits(A("qw", 0, 512)), T.wc[:], grp="w", after=["x%d" % len(CUT[0])])
    dma("y", A("sw", 0, 512), T.ws[:], grp="w")

    iota(A("idm"), [[1, 128]], 0, -1)
    iota(A("uli"), [[16, 8]], 0, small=False)
    iota(A("ci", 0, 32), [[0, 16], [1, 2]], 0, grp="ci")
    iota(A("ci", 64, 96), [[0, 2], [1, 8], [0, 2]], 0, grp="ci")
    iota(A("ci", 32, 48), [[32, 8], [C + 32, 2]], 0, grp="ci")
    iota(A("ci", 48, 64), [[32, 8], [-C, 2]], C + 16, grp="ci")
    iota(A("cei"), [[1, 4]], 4 * 192)
    iota(A("tfi", 0, 400), [[1, 400]], -192)
    iota(A("mi"), [[0, 24], [-1, 8]], 7)
    iota(A("tki", 0, 400), [[2, 200], [0, 2]], FRONT - 200)
    iota(A("lci"), [[1, 2], [256, 2]], 0)

    def unit(k):
        a = 3 - k if k < 4 else 527 - k
        quant("qz", "sz", 128 * k, 128 * k + 128, A("z", a, a + 512), grp="units%d" % (k // 4))

    fill(A("z"), 0.0)
    zeros = [(A("hi", 0, C, C - 1), 2), (A("kb", 0, 16), 16), (A("kb", C + 16, C + 32), 16), (A("fq", 0, 4 * C, C), 4)]
    for v, n in zeros + [(A("ts", PS * b, PS * b + FRONT + 2), FRONT + 2) for b in range(4)]:
        scal(v, A("idm", 0, n), 0.0, grp="fills")
    ts(A("z", 3, 515, 4), A("idm"), 0.0, 32.0, Op.is_equal, Op.mult)
    ts(A("z", 523, 1035, 4), A("idm"), 0.0, 0.25, Op.is_equal, Op.mult)
    copy(A("ul"), A("uli"))
    for k in range(6):
        unit(k)
    transp(A("ct"), A("ci"))
    quant("qu", "su", 0, 128, A("ub"))
    copy((T.qup[:, 0:128].bitcast(dt.uint32), A("qup")[1]), ind(A("qu", 0, 128), A("ul", 0, 8), word=True))
    scal(A("sup", 0, 128), ind(A("su", 0, 128), A("ul", 0, 8)))
    c_role, c_f, c_q = A("ct", 0, 1), A("ct", 32, 33), A("ct", 64, 65)
    c_sign, c_rb, c_none = A("cs", 0, 1), A("cs", 8, 9), A("cs", 16, 17)
    scal(c_sign, c_role, -2.0, 1.0)
    scal(A("ce"), A("cei"), 1.0 / 2048)
    scal(c_rb, c_role, 1.0 / 512)
    scal(c_none, c_role, 1.0 / 512, (NONE - 200) / 512)

    def score(t, j):
        a, b = runs_of(t)[j]
        bank = (4, 5)[j] if len(CUT[t]) == 1 else (0, 1, 5)[j]
        mm(bank, "qup", "sup", 0, "qx%d" % t, "sx%d" % t, a, b)
        scal(A("pb", a, b), P(bank, 0, b - a), c_sign)

    def rises(t, j):
        a, b = runs_of(t)[j]
        tt(A("gg", max(a, 1), b), A("pb", max(a, 1), b), A("pb", max(a, 1) - 1, b - 1), Op.is_gt)

    def peaks(a, b):
        tt(A("hi", a, b), A("gg", a, b), A("gg", a + 1, b + 1), Op.is_gt)

    def quant_run(t, j):
        a, b = runs_of(t)[j]
        quant("qx%d" % t, "sx%d" % t, a, b, A("xb%d" % t, XO + 4 * a, XO + 4 * b))

    scal(A("tf"), A("tfi"), 1.0 / 512)
    quant_run(0, 0)
    score(0, 0)
    quant_run(0, 1)
    score(0, 1)
    ts(A("mm"), A("mi"), c_q, None, Op.is_equal)
    unit(6)
    quant_run(0, 2)
    unit(7)

    for t in range(ROUNDS):
        xb, qx, sx = "xb%d" % t, "qx%d" % t, "sx%d" % t
        qn, sn, qe, se, ql, sl, e = ["%s%d" % (k, t) for k in ("qn", "sn", "qe", "se", "ql", "sl", "e")]
        nxb, nqx, nsx = "xb%d" % (t + 1), "qx%d" % (t + 1), "sx%d" % (t + 1)
        last = t == ROUNDS - 1
        tag = "r%d" % t
        runs = runs_of(t + 1)

        score(t, len(CUT[t]))
        for b in range(4):
            mm(b, "qz", "sz", 128 * b, qx, sx, 0, C)
        scal(A(xb, XO, XO + 4), A(xb, XO + 4 * C - 4, XO + 4 * C))
        if t == 0:
            scal(A("tk"), A("tki", 1, C + 1), 1.0 / 512, c_rb)
        ahead = 3 if t == 0 else 4
        for b in range(ahead):
            scal(win("fq", b, 1), P(b, 1, C), 1.0 / 128)

        H = CUT[t][-1]
        for j in range(len(CUT[t]) + 1):
            rises(t, j)
        peaks(1, H - 1)
        peaks(H - 1, C - 1)
        if last:
            for k in range(2):
                dma("y", A("oh", 32 * k, 32 * k + 24), (T.hi[k:128:16, :], A("hi")[1]), grp="oh")
        if t == 0:
            ts(A("lc"), A("lci"), c_f, float(2 * C + 31), Op.add, Op.min)
        scan(A("fb", 0, C - 1), A("hi", 0, C - 1), A("tf", 0, C - 1))
        scan(A("fb", C, 2 * C), A("hi", None, None, -1), A("tf", 1, C + 1))
        ts(A("eo", 0, 8, 2), A("ce"), A("fb", C - 2, C - 1), 2048.0, Op.add, Op.mult)
        scan(A("kb", 16, C + 16), A("hi"), A("tk"), c_none)
        scan(A("sel"), A("mm"), A("fb", C, 2 * C, 2))
        for c in range(4):
            (copy if c < 2 else scal)(A(xb, c, XO, 4), ind(A(xb, XO, XO + 4 * C), A("eo", 2 * c, 2 * c + 1)),
                                      grp=tag + "en")
        for b in range(ahead, 4):
            scal(win("fq", b, 1), P(b, 1, C), 1.0 / 128)
        ts(A("lb"), A("sel", 191, None, -8), -512.0, 192.0, Op.mult, Op.add)
        quant(qn, sn, 0, 128, A(xb, 0, 512))

        right = T.cores[(rank + 1) % n_ranks]
        n_end = len(topo.engines(T.cores[(rank - 1) % n_ranks], core))
        eng = topo.engines(core, right)
        rid, pid = topo.addr(right)[:2]
        half = len(eng) // 2

        def send_ends(qn=qn, sn=sn, qx=qx, sx=sx, t=t, eng=eng, half=half, rid=rid, pid=pid):
            d = DstId(rid=rid, pnc=pid)
            return g.remote_dma_fused([
                RemoteDMATransfer(dst_ids=[d], dma_engine_mask=_mask(eng[:half]), remote_sem=T.sem["ends%d" % t],
                                  src=T[qn][:, 0:4].bitcast(dt.uint8), dst=T[qx][:, C:C + 4].bitcast(dt.uint8)),
                RemoteDMATransfer(dst_ids=[d], dma_engine_mask=_mask(eng[half:]), remote_sem=T.sem["ends%d" % t],
                                  src=T[sn][:, 0:16], dst=T[sx][:, C:C + 16]),
            ], local_sem=T.sem.sent)

        rec("g", send_ends, [A(qn, 0, 4), A(sn, 0, 16)], [])
        sent[0] += len(eng)

        top = C - HELP[t]
        for b in range(3):
            scal(win("nx", b), ind(win("fq", b), A("lb")))
        if top:
            scal(win("nx", 3, 0, top), ind(win("fq", 3), A("lb", 0, top // 16)))
        for b in range(4):
            mm(4 + b, "qz", "sz", 512 + 128 * b, qx, sx, C + 4 - 128, C + 4,
               ext=[("ends%d" % t, n_end)] if b == 0 else [])

        def pairs(b):
            tt(A("ts", PS * b + FRONT + 2, PS * b + PS), win("nx", b, 0, C - 2), win("nx", b, 2, C), Op.add)

        ia, ic, most, least, down, low = [A("lf", a, a + 24) for a in (0, 32, 64, 96, 128, 160)]
        transp(A("tr", 0, C), A("kb", 16, C + 16), grp=tag + "tr")
        transp(A("tr", C, 2 * C + 32), A("kb"), grp=tag + "tr")
        copy(win("nx", 3, top, C), ind(win("fq", 3), A("lb", top // 16, C // 16)))
        ts(A("lf", 0, 64), ind(A("tr"), A("lc")), 512.0, 200.0, Op.mult, Op.add)
        pairs(0)
        tt(most, ia, ic, Op.max)
        tt(least, ia, ic, Op.min)
        pairs(1)
        ts(A("i2", 0, 24), most, float(FRONT), float(FRONT), Op.max, Op.subtract)
        ts(down, most, float(FRONT), float(BOTH - NONE), Op.is_lt, Op.mult)
        pairs(2)
        tt(low, least, down, Op.add)
        pairs(3)
        copy(A("i2", 32, 56), low)

        if last:
            tt(A("od"), A("oh", 0, 24), A("oh", 32, 56), Op.subtract)

        for b in range(4):
            tt(A("ts", PS * b + NONE, PS * b + NONE + 2), P(4 + b, 124, 126), win("nx", b, 0, 2), Op.add)
        for b in range(4):
            tt(A("ts", PS * b + BOTH, PS * b + BOTH + 1), A("ts", PS * b + NONE, PS * b + NONE + 1),
               A("ts", PS * b + NONE + 1, PS * b + NONE + 2), Op.add)

        if t == 0:
            dma("y", A("vb"), (T.v[:], A("ts", BOTH, BOTH + 1)[1]))

        mate = T.cores[rank ^ STEP[t]]
        eng = topo.engines(core, mate)
        rid, pid = topo.addr(mate)[:2]

        def second(j, b):
            a, b2 = runs[j]
            return ind(A("ts", PS * b, PS * b + PS), A("i2", 32 + a // 16, 32 + b2 // 16))

        def mean(j, planes):
            a, b2 = runs[j]
            for b in planes:
                tt(A(e, 4 * a + b, 4 * b2, 4), win("vv", b, a, b2) if (t, j, b) in PLAIN else second(j, b), win("uu", b, a, b2), Op.add)

        def send_mean(j):
            a, b2 = runs[j]
            quant(qe, se, a, b2, A(e, 4 * a, 4 * b2))
            for src, dst in ((bits(A(qe, a, b2)), bits(A(ql, a, b2))), (A(se, a, b2), A(sl, a, b2))):
                rec("g", lambda src=src, dst=dst, j=j, t=t, eng=eng, rid=rid, pid=pid: g.remote_dma(
                    dst[0], src[0], T.sem["mean%d_%d" % (t, j)], T.sem.sent, pid, rid, _mask(eng)), [src], [])
                sent[0] += len(eng)

        def mean32(j):
            a, b2 = runs[j]
            for b in range(4):
                scal(win("e32", b, a, b2), A(e, 4 * a + b, 4 * b2, 4), 32.0)

        def rest(j, planes):
            a, b2 = runs[j]
            for b in planes:
                tt(win("g32", b, a, b2), P(b, a, b2), win("e32", b, a, b2), Op.subtract)

        for j, (a, b2) in enumerate(runs):
            for b in range(4):
                scal(win("uu", b, a, b2), ind(A("ts", PS * b + FRONT, PS * b + PS), A("i2", a // 16, b2 // 16)))
                if last and a == 0 and b == 2:
                    scal(A("omv"), A("od"), 1.0, 1.0)
                    dma("y", T.om[:], A("omv"), grp="outy")
            if (t, j, 3) in PLAIN:
                scal(win("vv", 3, a, b2), second(j, 3))
        n = len(runs) - 1
        mean(0, range(4))
        for j in range(n):
            mean32(j)
            mean(j + 1, [0])
            send_mean(j)
            mean(j + 1, [1, 2, 3])
        mean32(n)
        rest(0, [0])
        send_mean(n)
        rest(0, [1, 2, 3])

        def product(j):
            a, b2 = runs[j]
            need = [("mean%d_%d" % (t, j), 2 * len(topo.engines(mate, core)))]
            for b in range(4):
                mm(4 * (1 - j % 2) + b, "qw", "sw", 128 * b, ql, sl, a, b2, ext=need if b == 0 else [])

        def state(j):
            a, b2 = runs[j]
            for b in range(4):
                tt(win("x32", b, a, b2), P(4 * (1 - j % 2) + b, 0, b2 - a), win("g32", b, a, b2), Op.add)
                if b < 3 or j < n:
                    scal(A(nxb, XO + 4 * a + b, XO + 4 * b2, 4), win("x32", b, a, b2), 1.0 / 32)

        def state_last():
            a, b2 = runs[n]
            ts(A(nxb, XO + 4 * a + 3, XO + 4 * b2, 4), win("x32", 3, a, b2), 1.0 / 32, None, Op.mult)

        H = runs[n][0]
        product(0)
        if last:
            rest(1, range(4))
            state(0)
            product(1)
            state(1)
            quant_run(t + 1, 0)
            mm(4, "qv", "sv", 0, nqx, nsx, 0, H)
            dma("y", T.oc[:, 0:4 * H], bits(A(nqx, 0, H)), grp="outy")
            state_last()
            scal(A("yb", 0, H), P(4, 0, H))
        else:
            rest(1, range(4))
            state(0)
            product(1)
            state(1)
            quant_run(t + 1, 0)
            state_last()
            score(t + 1, 0)
        quant_run(t + 1, n)
        if t == 0:
            quant("qv", "sv", 0, 128, A("vb"))
        if last:
            mm(5, "qv", "sv", 0, nqx, nsx, H, C)
            dma("y", T.oc[:, 4 * H:4 * C], bits(A(nqx, H, C)), grp="outy")
            for k in range(4):
                dma("y" if k < 2 else "a", T.osc[4 * k:4 * k + 4, 0:C],
                    (T[nsx][32 * k:32 * k + 4, 0:C], A(nsx, 0, C)[1]), grp="outy" if k < 2 else "outa")
            dma("y", T.y[:, 0:H], A("yb", 0, H), grp="outy")
            copy(A("yb", H, C), P(5, 0, C - H))
            dma("a", T.y[:, H:C], A("yb", H, C), grp="outa")

    rec("y", None, [], [], after=["outy"])
    rec("a", None, [], [], after=["outa"])
    rec("g", None, [], [], ext=[("sent", sent[0])])
    emit(ops, queues, T)
